import numpy as np, ml_dtypes
CORES = [6,15,38,47]
N = 4
import mx_ref
BF = ml_dtypes.bfloat16
def gentries(a):
    return np.ascontiguousarray(a.reshape(8, 16, -1).transpose(0, 2, 1)).reshape(8, -1)
def gtable(e):
    e = np.asarray(e); return np.ascontiguousarray(e.reshape(8, -1, 16).transpose(0, 2, 1)).reshape(128, -1).astype(np.int32)
def gcols(t, e):
    v = np.concatenate([t.reshape(8, 16, -1, 4), np.zeros((8, 16, 1, 4), BF)], axis=2)
    return np.ascontiguousarray(np.stack([v[g][:, e[g]] for g in range(8)])).reshape(128, -1)
def tile(rs):
    return np.stack(rs, axis=2).reshape(128, -1).astype(BF)
def cut(t, i, w=512):
    return t[:, w * i:w * i + w]
def pick(q, e):
    c = np.concatenate([q[0].reshape(128, -1, 4), np.zeros((128, 1, 4), np.uint8)], axis=1); s = np.concatenate([q[1], np.ones((16, 1), np.uint8)], axis=1)
    return (np.ascontiguousarray(c[:, e].reshape(128, -1)), np.ascontiguousarray(s[:, e]))
def join(*qs):
    return (np.concatenate([q[0] for q in qs], axis=1), np.concatenate([q[1] for q in qs], axis=1))
def put(q, e, v):
    c, s = q[0].reshape(128, -1, 4).copy(), q[1].copy(); c[:, e] = v[0].reshape(128, -1, 4); s[:, e] = v[1]
    return (c.reshape(128, -1), s)
def pk(c, s):
    return (np.ascontiguousarray(c), mx_ref.live(s))
def emit(q):
    return q[0], q[1]
def packed(v, rng):
    q = [mx_ref.quantize(np.ascontiguousarray(v[r])) for r in range(N)]
    return np.stack([a for a, b in q]), np.stack([mx_ref.plane(b, rng) for a, b in q])
def values_of_codes():
    e, c = np.zeros((128, 128, 4), np.float32), np.zeros((128, 2, 4), np.uint8)
    e[np.arange(128), np.arange(128), 0] = 1
    c[:127, :, 0] = np.arange(256).reshape(2, 128).T[:127]
    return mx_ref.matmul(mx_ref.quantize(e.reshape(128, 512).astype(BF)), (c.reshape(128, 8), np.full((16, 2), 127, np.uint8))).T.reshape(-1).astype(np.float64)
CODE_VALUE, SCALE_VALUE = values_of_codes(), 2.0 ** (np.arange(256) - 127.0)
def decode(q):
    return (CODE_VALUE[q[0]].reshape(16, 8, -1, 4) * SCALE_VALUE[q[1]][:, None, :, None] + 0.0).reshape(128, -1).astype(np.float32)
def f(rng, *shape):
    return mx_ref.flush((rng.standard_normal(shape, dtype=np.float32) * np.exp2(rng.integers(-2, 3, shape[:-1] + (1,)))).astype(BF))
def wide(rng, *shape, cols=0):
    v = rng.standard_normal(shape, dtype=np.float32) * np.exp2(rng.integers(-12, 13, shape)).astype(np.float32)
    if cols: v *= np.repeat(np.exp2(rng.integers(-cols, cols + 1, shape[:-2] + (1, shape[-1] // 4))) * (rng.random(shape[:-2] + (1, shape[-1] // 4)) > 0.0625), 4, axis=-1).astype(np.float32)
    return mx_ref.flush(v.astype(BF))
C, A, R = 320, 96, 2
def at(v, e):
    return np.take_along_axis(v, e, axis=1)
def bottleneck(s, up):
    c = np.abs(s - at(s, up))
    for i in range(9):
        c, up = np.maximum(c, at(c, up)), at(up, up)
    return c
def big(v):
    v = v.astype(np.float32)
    v[np.abs(v) < np.float32(2.0 ** -16)] = 0
    return v.astype(BF)
def numbers_of(rng):
    return {"x": big(f(rng, N, 128, 4 * C)), "u": np.array(f(rng, N, 128, 512)), "v": np.array(f(rng, N, 128, 512))}
def packed_layer(rng, w):
    c, p = packed(np.ascontiguousarray(w).reshape(N, 128, 2048), rng)
    return {"wc": c, "ws": p}
def weights(rng, still=[]):
    w = big(f(rng, N, 128, 2048)).reshape(N, 8, 16, 4, 8, 16, 4)
    for i in still:
        w[:, :, i] = 0
        w[:, :, :, :, :, i] = 0
    return packed_layer(rng, w)
def trees(rng):
    return rng.integers(0, np.maximum(np.arange(C), 1), (N, 8, C))
def places(rng):
    return np.stack([rng.integers(0, C + A * t, (N, 8, A, 4)) for t in range(R)], axis=2)
def lists_of(up, near):
    return {"pa": np.stack([gtable(up[r]) for r in range(N)]), "nr": np.stack([gtable(near[r].reshape(8, -1)) for r in range(N)])}
def signs(rng):
    return np.stack([rng.permutation(8) % 2 * 2.0 - 1.0 for r in range(N)])
def lost():
    t = np.zeros((128, 32, 4), np.float32)
    t[11, :, 0] = 4080
    t[8, :, 0] = 2.0 ** (11.0 - np.arange(32))
    once = decode(mx_ref.quantize(t.reshape(128, 128).astype(BF)))
    twice = decode(mx_ref.quantize(once.astype(BF)))
    e = np.flatnonzero((once[8, ::4] > 0) & (twice[8, ::4] == 0))
    return t[8, e[0] if len(e) else 16, 0]
def setup_inputs(rng):
    return {**numbers_of(rng), **weights(rng), **lists_of(trees(rng), places(rng))}
def setup_inputs_ties(rng):
    d = numbers_of(rng)
    e = rng.permutation(N)
    x = d["x"].reshape(N, 8, 16, C, 4)
    for r in range(N):
        k = np.zeros(C, int) if r == e[0] else rng.permutation(C) % 3
        a = x[r][:, :8, :3].copy()
        a[:, :, 2] = 0
        x[r][:, :8] = a[:, :, k]
    x[e[1]] = 0
    u = d["u"].reshape(N, 8, 16, 128, 4)
    u[:, :, 8:, ::16] = 0
    return {"x": x.reshape(N, 128, 4 * C), "u": u.reshape(N, 128, 512), "v": d["v"], **weights(rng, range(8)), **lists_of(trees(rng), places(rng))}
def setup_inputs_near(rng):
    d = numbers_of(rng)
    up, near = trees(rng), places(rng)
    x = d["x"].astype(np.float32).reshape(N, 8, 16, C, 4)
    x[:, :, 0] = 0
    x[:, :, 8:] = 0
    u = d["u"].reshape(N, 128, 128, 4)
    u[:, :, ::16] = 0
    o, c, j, half = rng.permutation(N) % 4, signs(rng), np.arange(C), C // 2
    for r in range(N):
        if o[r] == 3:
            up[r] = 0
            s = (j + rng.integers(A // 2, half, (8, 1))) % half
            x[r, :, 10, :, 0] = np.where(j < half, 9, 8) * 2.0 ** -30
        else:
            up[r] *= rng.integers(0, 2, (8, C))
            s = ((j + rng.integers(0, C, (8, 1))) % C + 1) // 2
        if o[r] < 2:
            x[r, :, 0, :, 0] = c[r][:, None]
            for g in rng.permutation(8)[:4]: x[r, g, 0, rng.integers(1, C), 0] *= np.float32(2.0 ** 30)
        b = ((s[:, :, None] >> np.arange(8)) & 1) * np.exp2(np.arange(8) - (23.0 if o[r] < 2 else 27.0))
        x[r, :, 8] = b[:, :, :4]
        x[r, :, 9] = b[:, :, 4:]
        k = 1.0 if o[r] == 0 else 2.0 ** -30
        for h in range(0, 128, 16):
            u[r, h, h, 0] = k
            u[r, h + 8:h + 10, h] = k
            u[r, h + 10, h, 0] = k
    x[:, :, 0, 0] = 0
    x[:, :, 8:, 0] = 0
    return {"x": x.reshape(N, 128, 4 * C).astype(BF), "u": u.reshape(N, 128, 512), "v": d["v"], **weights(rng, [0, 8, 9, 10, 11, 12, 13, 14, 15]), **lists_of(up, near)}
def setup_inputs_chains(rng):
    d = numbers_of(rng)
    up, near = trees(rng), places(rng)
    x = d["x"].astype(np.float32).reshape(N, 8, 16, C, 4)
    x[:, :, 8:] = 0
    u = d["u"].reshape(N, 128, 128, 4)
    u[:, :, ::16] = 0
    j = np.arange(C)
    chain, zig, h = np.maximum(j - 1, 0), 1 - 2 * (j % 2), rng.permutation(8)
    k = np.where(rng.permutation(N) < N // 2, 2.0 ** -30, 1.0)
    small = lost()
    p = int(rng.integers(N))
    for r in range(N):
        o = (r - p) % N
        s = rng.integers(0, 1000, (8, C))
        s[h[0], 0] = 4095
        s[h[1]] = 2048 + zig * ((C - j) // 2)
        s[h[2]] = 2048 + zig * ((j + 1) // 2)
        if o < 2:
            s[h[3]] = np.where(j <= A // 2, 1600 + zig * (599 + j), 1600)
            s[h[3], 0] = 0
        s[h[4]] = np.where(j < C // 2, 7, 3000)
        s[h[6]] = rng.integers(0, 8, C)
        s[h[7]] = 0
        up[r, h[:5]] = chain
        up[r, h[5]] = 0
        up[r, h[6]] = np.minimum(chain, C // 2)
        b = ((s[:, :, None] >> np.arange(12)) & 1) * np.exp2(np.arange(12.0))
        for i in range(3): x[r, :, 8 + i] = b[:, :, 4 * i:4 * i + 4]
        x[r, h[7], 8, 1:, 0] = small
        x[r, h[7], 11, :, 0] = 4080
        near[r, h[7], :, :, 0] = rng.integers(1, C, (R, A))
        near[r, h[7], :, :, 1] = 0
        near[r, h[7], 0, A // 2:] = rng.integers(1, C, (A - A // 2, 4))
        own = h[3] if o == 1 else h[5] if o == 3 else h[7]
        m = rng.permutation(h[:7][h[:7] != own])
        near[r, m[0]] = near[r, m[0], :, :1].copy()
        near[r, m[1]] = near[r, m[1], :, :, :1].copy()
        near[r, m[2]] = 0
        near[r, m[3]] = C - 1
        for t in range(R): near[r, m[4], t] = np.resize(rng.permutation(C + A * t), 4 * A).reshape(A, 4)
        near[r, m[5], 1] = C + rng.integers(0, A, (A, 4))
        for i in range(0, 128, 16): u[r, i + 8:i + 11, i] = k[r]
        if o == 1:
            near[r, h[3], 0] = 0
            near[r, h[3], 0, A // 2 + 1:] = np.arange(2, A // 2 + 1)[:, None] - np.array([1, 0, 1, 0])
        if o == 2:
            x[r, h[5], 8:] = 0
            x[r, h[5], 9, 1:, 0] = 10 * 2.0 ** -32
        if o == 3:
            x[r, h[5], 8:] = 0
            x[r, h[5], 8, 1:, 0] = 9 * 2.0 ** -32
            i = 16 * int(h[5])
            u[r, i + 8, i] = 9 * 2.0 ** -33
            u[r, i + 9:i + 11, i] = 2.0 ** -30
            near[r, h[5], 0, :, 0] = 0
    return {"x": x.reshape(N, 128, 4 * C).astype(BF), "u": u.reshape(N, 128, 512), "v": d["v"], **weights(rng, range(8, 16)), **lists_of(up, near)}
def setup_inputs_huge(rng):
    d = numbers_of(rng)
    up = trees(rng)
    c = np.stack([rng.permutation(C) % 2 * 2.0 - 1.0 for r in range(N)])
    c[rng.permutation(N) < N // 2] = -1
    for r in range(N):
        if (c[r] > 0).any():
            c[r, 1:3] = 1, -1
            e = np.where(c[r] > 0, 2, 1)
            e[:3] = 0, 0, 1
            up[r, rng.permutation(8)[:4]] = e
    x = (0.8 + 0.2 * rng.random((N, 128, C, 4))) * np.where(c < 0, -2.0 ** 30, 0.4 * 2.0 ** 30)[:, None, :, None]
    x[:, :, 0] = 0
    u = d["u"].reshape(N, 128, 128, 4)
    a = 2.0 ** 30 * (1 - 0.125 * rng.random((N, 128, 8, 4))) * signs(rng)[:, None, :, None]
    u[:, :, ::16] = a.astype(np.float32).astype(BF)
    w = np.zeros((N, 128, 4, 128, 4), np.float32)
    i = np.arange(128)
    for b in range(4): w[:, i, b, i, b] = 16
    return {"x": x.astype(np.float32).reshape(N, 128, 4 * C).astype(BF), "u": u.reshape(N, 128, 512), "v": d["v"], **packed_layer(rng, w.astype(BF)), **lists_of(up, places(rng))}
def setup_inputs_spread(rng):
    d = setup_inputs(rng)
    d["x"] = big(wide(rng, N, 128, 4 * C, cols=6))
    return d
def check_inputs(d):
    b = []
    for k in ("x", "u", "v"):
        a = np.abs(d[k].astype(np.float32))
        if not (np.isfinite(a).all() and ((a == 0) | (a >= 2.0 ** -30) & (a <= 2.0 ** 30)).all()): b.append("a value of " + k)
    none, least, most = [emit(mx_ref.quantize(np.full((128, 16), k, np.float32).astype(BF)))[1][0, 0] for k in (0.0, 2.0 ** -30, 2.0 ** 30)]
    for r in range(N):
        if ((d["wc"][r] == 0x7F) | (d["wc"][r] == 0xFF)).any(): b.append("wc: a code that is no number")
        s = mx_ref.live(d["ws"][r])
        if ((s != none) & ((s < least) | (s > most))).any(): b.append("ws: a scale out of range")
        e = gentries(d["pa"][r])
        if ((e < 0) | (e > np.maximum(np.arange(C) - 1, 0))).any(): b.append("pa: a parent out of range")
        e = gentries(d["nr"][r]).reshape(8, R, 4 * A)
        if ((e < 0) | (e >= C + A * np.arange(R)[:, None])).any(): b.append("nr: a near place out of range")
    return b
def reference(x, u, v, wc, ws, pa, nr):
    qu = [mx_ref.quantize(u[r]) for r in range(N)]
    lay = [pk(wc[r], ws[r]) for r in range(N)]
    now = [x[r] for r in range(N)]
    up = [gentries(pa[r]) for r in range(N)]
    near = [gentries(nr[r]).reshape(8, R, A, 4) for r in range(N)]
    for t in range(R):
        n = C + A * t
        sent, s, c = [], [], []
        for r in range(N):
            s.append(mx_ref.matmul(qu[r], mx_ref.quantize(now[r]))[::16])
            c.append(bottleneck(s[r], up[r]))
            sent.append(mx_ref.quantize(gcols(now[r], np.argsort(c[r], axis=1, kind="stable")[:, :A])))
        came = decode(join(*sent)).astype(BF)
        for r in range(N):
            new = np.ascontiguousarray(cut(came, (r - 1) % N, 4 * A))
            k = mx_ref.matmul(qu[r], mx_ref.quantize(new))[::16]
            i = near[r][:, t].reshape(8, 4 * A)
            gap = np.abs(at(s[r], i) - np.repeat(k, 4, axis=1))
            cost = np.maximum(at(c[r], i), gap).reshape(8, A, 4)
            parent = np.take_along_axis(near[r][:, t], np.argmin(cost, axis=2)[:, :, None], axis=2)[:, :, 0]
            price = np.maximum(np.repeat(np.min(cost, axis=2), 4, axis=1), gap)
            all_prices = np.full((8, n, A), np.inf, np.float32)
            for g in range(8): all_prices[g, i[g], np.arange(4 * A) // 4] = price[g]
            moved = np.min(all_prices, axis=2) < c[r]
            up[r] = np.concatenate([np.where(moved, n + np.argmin(all_prices, axis=2), up[r]), parent], axis=1)
            z = np.concatenate([now[r], new], axis=1)
            q = mx_ref.quantize(((z.astype(np.float32) + gcols(z, up[r]).astype(np.float32)) * np.float32(0.5)).astype(BF))
            now[r] = tile([np.maximum(mx_ref.matmul(pick(lay[r], np.arange(128 * b, 128 * b + 128)), q), np.float32(0.0)) * np.float32(0.03125) + z[:, b::4].astype(np.float32) for b in range(4)])
    n = C + A * R
    y, op = np.zeros((N, 128, n), np.float32), np.zeros((N, 8, n), np.float32)
    oc, osc = np.zeros((N, 128, 4 * n), np.uint8), np.zeros((N, 16, n), np.uint8)
    for r in range(N):
        q = mx_ref.quantize(now[r])
        y[r] = mx_ref.matmul(mx_ref.quantize(v[r]), q)
        op[r] = up[r]
        oc[r], osc[r] = emit(q)
    return {"y": y, "op": op, "oc": oc, "osc": osc}

@@ -1,0 +1,704 @@
+from concourse.mybir import dt, AluOpType, ActivationFunctionType
+
+AL = AluOpType
+AF = ActivationFunctionType
+C, A, R = 320, 96, 2
+SL = 4 * A
+BIG, HUGE = 1e29, 5e29
+RADIX = [[3, 3, 4, 0], [3, 3, 3, 4, 4]]
+STEP = 32
+BOTH = [[], [22, 18, 14]]
+CHUNKS = [[(0, 192), (192, 416)], [(0, 320), (320, 512)]]
+LAT, DMA_LAT, FAR_LAT = 130, 2600, 3000
+TRIES = 600
+
+BYTES = {"float32": 4, "int32": 4, "bfloat16": 2, "uint16": 2, "uint8": 1, "float8_e4m3fn_x4": 4}
+ARENA = {}
+PLACE = {}
+
+
+def region(name, buf, dtype, cols):
+    if buf not in ARENA:
+        ARENA[buf] = [dtype, 0]
+    al = 32 // BYTES[dtype]
+    off = (ARENA[buf][1] + al - 1) // al * al
+    PLACE[name] = (buf, off, cols)
+    ARENA[buf][1] = off + cols
+
+
+def shared(name, t, buf, dtype, cols):
+    if t == R - 1:
+        region(name + str(t), buf, dtype, cols)
+    else:
+        last = PLACE[name + str(R - 1)]
+        PLACE[name + str(t)] = (last[0], last[1], cols)
+
+
+def own(name, dtype, cols):
+    region(name, name, dtype, cols)
+
+
+def pair(name, cols):
+    own(name + "c", "float8_e4m3fn_x4", cols)
+    own(name + "s", "uint8", cols)
+
+
+def planes_of(n):
+    pl = list(range(1, n // 16)) + ["D"]
+    pl = [None] * (-len(pl) % 4) + pl
+    return [pl[i:i + 4] for i in range(0, len(pl), 4)]
+
+
+def width(p, n):
+    return 0 if p is None else n if p == "D" else 16 * p
+
+
+F, B, I, U = "float32", "bfloat16", "int32", "uint16"
+for _n, _c in (("ones", 512), ("iota", 512), ("mod16", 512), ("mask", 512), ("rst", 512), ("offd", 512), ("r4", SL),
+               ("blk", 512), ("hugeb", 32)):
+    region(_n, "kb", B, _c)
+for _n, _c in (("rf", 1), ("gf", 1), ("hit", 512), ("cb", 4), ("bkt", 4), ("dum", 4), ("slw", 48),
+               ("plw", 32), ("left0", 32), ("left1", 32)):
+    region(_n, "kf", F, _c)
+for _n, _c in (("pi", 1), ("ri", 1), ("gi", 1), ("upi", 8)):
+    region(_n, "ki", I, _c)
+own("upo", U, 8)
+for _b in range(4):
+    region("et%d" % _b, "kt", B, 512)
+region("bd", "kt", B, 512)
+pair("eq", 512)
+pair("bdq", 128)
+own("ut", B, 512)
+own("vt", B, 512)
+pair("uq", 128)
+pair("ur", 128)
+pair("vq", 128)
+pair("wq", 512)
+own("pw0", I, 32)
+own("nri", I, 48)
+region("nro", "ou", U, 48)
+region("endo", "ou", U, 4)
+for _n, _c in (("key", 2 * SL), ("nu0", SL), ("nu1", SL), ("near0", SL), ("near1", SL), ("nkey", 48), ("hi2", 48), ("cnt", 8),
+               ("e1", 4), ("e2", 4), ("e3", 4), ("e4", 4), ("em", 4), ("opr", 512)):
+    region(_n, "xf", F, _c)
+region("hi1", "xi", I, 48)
+own("x2", B, 2048)
+pair("q2", 512)
+own("ysb", F, 512)
+for _t in range(R - 1, -1, -1):
+    _n = C + A * _t
+    _s = str(_t)
+    own("x" + _s, B, 4 * (_n + A))
+    pair("q" + _s, _n)
+    pair("l" + _s, _n)
+    pair("h" + _s, 128)
+    pair("yq" + _s, _n + A)
+    own("el" + _s, U, 8)
+    own("es" + _s, U, 8)
+    shared("yt", _t, "yt", B, 4 * (_n + A))
+    region("pw" + str(_t + 1), "xi", I, 32)
+    region("po" + _s, "ou", U, 32)
+    for _b in range(4):
+        region("xh%d%d" % (_t, _b), "xh" + _s, B, _n + A)
+        shared("xo%d" % _b, _t, "xo", B, _n + A)
+        region("dp%d%d" % (_t, _b), "dp" + _s, B, _n)
+        shared("rl%d" % _b, _t, "rl", F, _n + A)
+    for _x, _c in (("s", _n), ("sp", _n), ("ce", _n), ("sm", _n), ("df", _n), ("ca", _n), ("cc", _n), ("cd", _n), ("cm", _n),
+                   ("hold", 512), ("sn", SL), ("snm", SL), ("cn", SL), ("d1", SL), ("d2", SL), ("gap", SL), ("gaps", SL),
+                   ("cost", SL), ("f4", SL + 8), ("price", SL), ("fs", 424)):
+        if _x in ("d1", "d2", "gap", "gaps", "cost", "price", "df", "cm", "sm", "cc", "cd", "sp", "ce"):
+            shared(_x, _t, "sc", F, _c)
+        else:
+            region(_x + _s, "sc", F, _c)
+    for _x, _c in (("rs", 32), ("colm", _n), ("cols", _n), ("r1", 32), ("r2", 32), ("r3", 32), ("sg", 24), ("a4", SL), ("pm", A),
+                   ("ps", A), ("us", SL), ("as", 424), ("mv", 32), ("dl", 32), ("dm", 32)):
+        region(_x + _s, "xf", F, _c)
+    for _x, _c in (("wa", _n), ("wb", _n), ("wc", _n), ("gm", _n), ("gs", _n), ("dgs", _n), ("ew", _n), ("em", A), ("ec", A),
+                   ("sw", SL), ("swm", SL), ("sws", SL), ("keep", SL), ("nf", SL), ("rr", 448)):
+        region(_x + _s, "xb", B, _c)
+    for _x, _c in (("si", 24), ("sh", 24), ("pp", 8)):
+        region(_x + _s, "xi", I, _c)
+    for _x, _c in (("rk", 32), ("pos", 24), ("so", 24), ("do", 24)):
+        region(_x + _s, "ou", U, _c)
+    for _k in range(1, len(RADIX[_t])):
+        region("ql%d%d" % (_t, _k), "ou", U, 32)
+    for _m, _pl in enumerate(planes_of(_n)):
+        _w = max(128, width(_pl[3], _n))
+        region("tl%d%d" % (_t, _m), "tl" + _s, B, 4 * _w)
+        region("tc%d%d" % (_t, _m), "tc" + _s, "float8_e4m3fn_x4", _w)
+        region("ts%d%d" % (_t, _m), "ts" + _s, "uint8", _w)
+    shared("jr", _t, "jrow", B, 8 * (_n // 16) * (_n // 16))
+    shared("js", _t, "junk", B, 6 * SL)
+region("po2", "ou", U, 32)
+region("jc", "junk", B, 4 * SL)
+
+SCRATCH = {}
+for _k, _v in ARENA.items():
+    SCRATCH[_k] = ("sbuf", [128, _v[1] + _v[1] % 2], _v[0])
+SCRATCH["acc"] = ("psum", [128, 4096], "float32")
+PLACE["acc"] = ("acc", 0, 4096)
+
+LOADS = ["lx", "lu", "lpa", "lnr", "lwc", "lws", "lv"]
+FAR = ["ac0", "ac1", "al0", "al1"]
+SEMAPHORES = ["cV", "cS", "cT", "cG", "out", "sent", "xo0", "xo1"] + LOADS + FAR
+
+
+def v(name, a=0, b=None, s=1):
+    return (name, a, PLACE[name][2] if b is None else b, s)
+
+
+def count(x):
+    return len(range(x[1], x[2], x[3]))
+
+
+def wide(x):
+    return 4 if x[0] == "acc" else BYTES[ARENA[PLACE[x[0]][0]][0]]
+
+
+def bank(k, a, b, s=1):
+    return ("acc", 512 * k + a, 512 * k + b, s)
+
+
+def build(g, T, topo, dst):
+    ops = []
+    rid, pid, _se = topo.addr(dst[1])
+    far_mask = topo.mask(dst[0], dst[1])
+    far_n = len(topo.engines(dst[0], dst[1]))
+
+    def ap(x):
+        buf, off, _c = PLACE[x[0]]
+        if x[3] == 1:
+            return T[buf][:, off + x[1]:off + x[2]]
+        return T[buf][:, off + x[1]:off + x[2]:x[3]]
+
+    def src(x):
+        if x[0] == "@":
+            return ap(x[1]).indirect(ap(x[2]))
+        return ap(x)
+
+    def rd(x):
+        if isinstance(x, tuple):
+            return [x[1], x[2]] if x[0] == "@" else [x]
+        return []
+
+    def sc(x):
+        return ap(x) if isinstance(x, tuple) else x
+
+    def add(q, fn, reads, writes, cost, sem=None, inc=1, lat=LAT):
+        ops.append({"q": q, "fn": fn, "r": reads, "w": writes, "cost": cost, "sem": sem, "inc": inc, "lat": lat})
+
+    def at(win, off):
+        return ("@", win, off)
+
+    def vcost(out, ins, two):
+        n = count(out)
+        if ins[0][0] == "@":
+            return 60 + 1.56 * n
+        if two:
+            return max(64, n * (1 if any(x[0] == "acc" for x in ins) else 2))
+        return max(64, n * (0.5 if all(wide(x) == 2 for x in ins + [out]) else 1))
+
+    def tt(out, a, b, op):
+        add("V", lambda: g.vector.tensor_tensor(ap(out), src(a), ap(b), op), rd(a) + [b], [out], vcost(out, [a, b], True))
+
+    def ts(out, a, s1, op0, s2=None, op1=None):
+        if op1 is None:
+            fn = lambda: g.vector.tensor_scalar(ap(out), src(a), sc(s1), None, op0)
+        else:
+            fn = lambda: g.vector.tensor_scalar(ap(out), src(a), sc(s1), sc(s2), op0, op1)
+        add("V", fn, rd(a) + rd(s1) + rd(s2), [out], vcost(out, [a], False))
+
+    def cp(out, a):
+        add("V", lambda: g.vector.tensor_copy(ap(out), src(a)), rd(a), [out], vcost(out, [a], False))
+
+    def scatter(win, off, a):
+        add("V", lambda: g.vector.tensor_copy(ap(win).indirect(ap(off)), ap(a)), [a, off], [win], 60 + 3.8 * count(a))
+
+    def scan(out, d0, d1, init, op0, op1):
+        add("V", lambda: g.vector.tensor_tensor_scan(ap(out), ap(d0), ap(d1), init, op0, op1), [d0, d1], [out],
+            vcost(out, [d0, d1], False))
+
+    def fill(out, c):
+        add("V", lambda: g.vector.memset(ap(out), c), [], [out], max(64, count(out) * wide(out) / 4))
+
+    def quant(qc, qs, x):
+        add("V", lambda: g.vector.quantize_mx(ap(qc), ap(qs), ap(x)), [x], [qc, qs], 15 + 0.27 * count(x))
+
+    def act(out, a, f, bias=None, scale=None, acc=None):
+        kw = {}
+        if bias is not None:
+            kw["bias"] = bias
+        if scale is not None:
+            kw["scale"] = scale
+        if acc is not None:
+            kw["accum_out"] = acc
+        n = count(out)
+        cost = (80 + 1.56 * n if a[0] == "@" else 60 + n) + (25 if acc else 0)
+        add("S", lambda: g.scalar.activation(ap(out), src(a), f, **{k: sc(x) for k, x in kw.items()}),
+            rd(a) + rd(bias), [out] + rd(acc), cost)
+
+    def iota(out, pat, base, cm):
+        if ARENA[PLACE[out[0]][0]][0] == I:
+            fn = lambda: g.iota(ap(out), pat, base, cm)
+        else:
+            fn = lambda: g.iota(ap(out), pat, base, cm, allow_small_or_imprecise_dtypes=True)
+        add("G", fn, [], [out], 160 + 2 * count(out))
+
+    def zero(out):
+        iota(out, [[0, count(out)]], 0, 0)
+
+    def mm(out, wc, ws, xc, xs, start=True, stop=True):
+        add("T", lambda: g.tensor.matmul_mx(ap(out), ap(wc), ap(ws), ap(xc), ap(xs), start, stop), [wc, ws, xc, xs], [out],
+            (count(out) + 16) * 1.2)
+
+    def dma(q, fn, reads, writes, sem, lat=DMA_LAT):
+        e = g.sync if q == "Y" else g.scalar
+        add(q, lambda: fn(e), reads, writes, 80, sem, 16, lat)
+
+    def far(out, a, sem, codes, lat):
+        if codes:
+            fn = lambda: g.remote_dma(ap(out).bitcast(dt.uint8), ap(a).bitcast(dt.uint8), T.sem[sem], T.sem.sent, pid, rid, far_mask)
+        else:
+            fn = lambda: g.remote_dma(ap(out), ap(a), T.sem[sem], T.sem.sent, pid, rid, far_mask)
+        add("G", fn, [a], [out], 600, sem, far_n, lat)
+
+    def wrap(spread, n, tmp):
+        scan(v(tmp, 0, n), v("rst", 0, n), spread, 0.0, AL.mult, AL.add)
+        return v(tmp, 15, n, 16)
+
+    dma("S", lambda e: e.dma_start(ap(v("pw0", 0, 20)), T.pa[:]), [], [v("pw0", 0, 20)], "lpa")
+    dma("Y", lambda e: e.dma_start(ap(v("ut")), T.u[:]), [], [v("ut")], "lu")
+    dma("Y", lambda e: e.dma_start(ap(v("x0", 0, 4 * C)), T.x[:]), [], [v("x0", 0, 4 * C)], "lx", DMA_LAT + 600)
+    dma("S", lambda e: e.dma_start(ap(v("nri")), T.nr[:]), [], [v("nri")], "lnr")
+    dma("Y", lambda e: e.dma_start(ap(v("wqc")).bitcast(dt.uint8), T.wc[:]), [], [v("wqc")], "lwc")
+    dma("Y", lambda e: e.dma_start(ap(v("wqs")), T.ws[:]), [], [v("wqs")], "lws")
+    dma("Y", lambda e: e.dma_start(ap(v("vt")), T.v[:]), [], [v("vt")], "lv")
+
+    iota(v("pi"), [[0, 1]], 0, 1)
+    iota(v("mod16"), [[0, 32], [1, 16]], 0, 0)
+    iota(v("upi"), [[16, 8]], 0, 0)
+    iota(v("hit"), [[512, 32], [0, 16]], 0, 0)
+    iota(v("plw"), [[16, 32]], 0, 0)
+    iota(v("cb"), [[1, 2], [16, 2]], 0, 0)
+    iota(v("blk"), [[1, 8], [0, 64]], 0, 0)
+    fill(v("ones"), 1.0)
+    scan(v("iota"), v("ones"), v("ones"), -257.0, AL.mult, AL.add)
+    ts(v("ri"), v("pi"), 15, AL.bitwise_and)
+    cp(v("rf"), v("ri"))
+    ts(v("gi"), v("pi"), 4, AL.arith_shift_right)
+    cp(v("gf"), v("gi"))
+    ts(v("mask"), v("mod16"), v("rf"), AL.is_equal)
+    ts(v("rst"), v("mod16"), 0.5, AL.is_gt)
+    ts(v("offd"), v("mod16"), v("rf"), AL.not_equal, BIG, AL.mult)
+    zero(v("r4"))
+    ts(v("r4", 0, SL, 4), v("ones", 0, A), HUGE, AL.mult)
+    fill(v("hugeb"), HUGE)
+    cp(v("upo"), v("upi"))
+    for b in range(4):
+        add("G", lambda b=b: g.affine_select(ap(v("et%d" % b)), ap(v("ones")), [[-1, 512]], AL.is_equal, 0.0, b, 4),
+            [v("ones")], [v("et%d" % b)], 1230)
+        quant(v("eqc", 128 * b, 128 * b + 128), v("eqs", 128 * b, 128 * b + 128), v("et%d" % b))
+    ts(v("bd"), v("blk"), v("gf"), AL.is_equal)
+    quant(v("bdqc"), v("bdqs"), v("bd"))
+    for t in range(R):
+        ts(v("slw", 24 * t, 24 * t + 24), v("plw", 0, 24), v("rf"), AL.add, -256.0, AL.add)
+    quant(v("uqc"), v("uqs"), v("ut"))
+    add("V", lambda: g.vector.tensor_copy(ap(v("urc")).bitcast(dt.uint32), ap(v("uqc")).bitcast(dt.uint32).indirect(ap(v("upo")))),
+        [v("uqc"), v("upo")], [v("urc")], 260)
+    add("S", lambda: g.scalar.activation(ap(v("urs")), ap(v("uqs")).indirect(ap(v("upo"))), AF.Copy),
+        [v("uqs"), v("upo")], [v("urs")], 280)
+    quant(v("vqc"), v("vqs"), v("vt"))
+
+    cp(v("nro"), v("nri"))
+    for t in range(R):
+        tt(v("key", SL * t, SL * t + SL), at(v("hit"), v("nro", 24 * t, 24 * t + 24)), v("iota", 0, SL), AL.add)
+    ts(v("hi1"), v("nri"), 4, AL.arith_shift_right)
+    ts(v("hi2"), v("hi1"), -512.0, AL.mult)
+    tt(v("nkey"), v("hi2"), v("slw"), AL.subtract)
+    ts(v("bkt"), v("cb"), v("rf"), AL.add, -512.0, AL.mult)
+    ts(v("bkt"), v("bkt"), 300.0, AL.add)
+    for t in range(R):
+        ts(v("dum", 2 * t, 2 * t + 2), v("cb", 0, 2), v("rf"), AL.add, 385.0, AL.add)
+        for i in range(4):
+            col = 4 * (i // 2) + 2 * t + i % 2
+            act(v("jc", SL * i, SL * i + SL), v("key", SL * t, SL * t + SL), AF.Sign, bias=v("bkt", i, i + 1),
+                acc=v("cnt", col, col + 1))
+    ts(v("e1"), v("cnt", 0, 4), 0.5, AL.mult, 191.0, AL.add)
+    tt(v("em"), v("cnt", 0, 4), v("cnt", 4, 8), AL.is_equal)
+    tt(v("e2"), v("dum"), v("e1"), AL.subtract)
+    tt(v("e3"), v("e2"), v("em"), AL.mult)
+    tt(v("e4"), v("e3"), v("e1"), AL.add)
+    cp(v("endo"), v("e4"))
+    for t in range(R):
+        act(v("near%d" % t), at(v("iota"), v("nro", 24 * t, 24 * t + 24)), AF.Identity, bias=256.0)
+        for i in range(4):
+            act(v("nu%d" % t, i, SL, 4), v("near%d" % t, i, SL, 4), AF.Identity, bias=512.0 * (3 - i))
+    zero(v("pw0", 20, 32))
+    zero(v("pw1", 24, 32))
+    cp(v("po0", 0, 20), v("pw0", 0, 20))
+
+    for t in range(R):
+        n = C + A * t
+        K = n // 16
+        s = str(t)
+        m = n + A
+        nro = v("nro", 24 * t, 24 * t + 24)
+        for c in range(24):
+            act(v("js" + s, SL * (c % 6), SL * (c % 6) + SL), v("key", SL * t, SL * t + SL), AF.Sign,
+                bias=v("nkey", 24 * t + c, 24 * t + c + 1), acc=v("sg" + s, c, c + 1))
+        ts(v("pos" + s), v("sg" + s), 383.0, AL.add, 0.5, AL.mult)
+        scatter(v("sw" + s), v("pos" + s), v("iota", 0, SL))
+        tt(v("swm" + s), v("sw" + s), v("mask", 0, SL), AL.mult)
+        w = wrap(v("swm" + s), SL, "sws" + s)
+        ts(v("so" + s), w, 256.0, AL.add)
+        ts(v("si" + s), w, 256.0, AL.add)
+        ts(v("sh" + s), v("si" + s), 2, AL.arith_shift_right)
+        ts(v("do" + s), v("sh" + s), 4.0, AL.mult, 3.0, AL.add)
+        act(v("us" + s), at(v("iota"), v("do" + s)), AF.Identity, bias=63.25 + n, scale=0.25)
+        zero(v("rr" + s))
+        scatter(v("rr" + s, 16, 448), v("endo", 2 * t, 2 * t + 2), v("hugeb"))
+        fill(v("fs" + s, SL, 424), BIG)
+        zero(v("as" + s, SL, 424))
+        zero(v("keep" + s))
+        zero(v("hold" + s, n, 512))
+        zero(v("rs" + s, 0, 1))
+        ts(v("left" + s), v("plw"), -1.0, AL.mult, v("rf"), AL.add)
+        tiles = planes_of(n)
+        for k, pl in enumerate(tiles):
+            lo, hi = width(pl[0], n), max(128, width(pl[3], n))
+            zero(v("tl%d%d" % (t, k), 4 * lo, 4 * hi))
+
+        qc, qs = v("q%dc" % t), v("q%ds" % t)
+        if t == 0:
+            quant(qc, qs, v("x0", 0, 4 * n))
+        far(v("l%dc" % t), qc, "ac" + s, True, FAR_LAT + 1500)
+        far(v("l%ds" % t), qs, "ac" + s, False, FAR_LAT + 1500)
+        mm(bank(4, 0, n), v("urc"), v("urs"), qc, qs)
+        cp(v("s" + s), bank(4, 0, n))
+        act(v("sp" + s), at(v("s" + s), v("po" + s, 0, K)), AF.Copy)
+        tt(v("df" + s), bank(4, 0, n), v("sp" + s), AL.subtract)
+        act(v("ca" + s), v("df" + s), AF.Abs)
+        act(v("ce" + s), v("df" + s), AF.Abs)
+        tt(v("sm" + s), bank(4, 0, n), v("offd", 0, n), AL.add)
+        act(v("sn" + s), at(v("s" + s), nro), AF.Copy)
+        act(v("snm" + s), at(v("sm" + s), nro), AF.Copy)
+        for b in range(4):
+            act(v("xh%d%d" % (t, b), 0, n), v("x" + s, b, 4 * n, 4), AF.Copy, scale=0.5)
+            dma("Y", lambda e, b=b, t=t, n=n: e.dma_start(ap(v("xo%d%d" % (b, t), 0, n)), ap(v("xh%d%d" % (t, b), 0, n))),
+                [v("xh%d%d" % (t, b), 0, n)], [v("xo%d%d" % (b, t), 0, n)], "xo" + s)
+            mm(bank(b, 0, n), v("eqc", 128 * b, 128 * b + 128), v("eqs", 128 * b, 128 * b + 128), v("l%dc" % t), v("l%ds" % t))
+            act(v("dp%d%d" % (t, b)), bank(b, 0, n), AF.Copy)
+
+        lst = v("po" + s, 0, K)
+        wins = ["wa" + s, "wb" + s, "wc" + s]
+        act(v(wins[0]), at(v("iota"), lst), AF.Copy)
+        cs = ["ca" + s, "cc" + s, "cd" + s]
+        for k, rho in enumerate(RADIX[t]):
+            if k + 1 < len(RADIX[t]):
+                for j in range(rho - 2):
+                    act(v(wins[1]), at(v(wins[0]), lst), AF.Copy)
+                    wins = wins[1:] + wins[:1]
+                tt(v("gm" + s), at(v(wins[0]), lst), v("mask", 0, n), AL.mult)
+                w = wrap(v("gm" + s), n, "gs" + s)
+                nxt = v("ql%d%d" % (t, k + 1), 0, K)
+                ts(nxt, w, 256.0, AL.add)
+                if k + 2 < len(RADIX[t]):
+                    act(v(wins[1]), at(v(wins[0]), lst), AF.Copy)
+                    wins = wins[1:] + wins[:1]
+            if rho == 0:
+                for a in range(STEP, n, STEP):
+                    tt(v(cs[0], a, a + STEP), at(v(cs[0], 0, a), (lst[0], a // 16, (a + STEP) // 16, 1)), v(cs[0], a, a + STEP), AL.max)
+            elif k > 0:
+                act(v("ce" + s), v(cs[0]), AF.Copy)
+            for j in range(rho - 1):
+                tt(v(cs[1]), at(v(cs[0]), lst), v("ce" + s), AL.max)
+                cs = cs[1:] + cs[:1]
+            if k + 1 < len(RADIX[t]):
+                lst = nxt
+        c = cs[0]
+        act(v("cn" + s), at(v(c), nro), AF.Copy)
+
+        tt(v("cm" + s), v(c), v("mask", 0, n), AL.mult)
+        scan(v("hold" + s, 0, n), v("rst", 0, n), v("cm" + s), 0.0, AL.mult, AL.add)
+        used = 0
+        for k in range(len(tiles) - 1, -1, -1):
+            tl = "tl%d%d" % (t, k)
+            hi = max(128, width(tiles[k][3], n))
+            for j in range(3, -1, -1):
+                p = tiles[k][j]
+                if p == "D":
+                    tt(v(tl, j, 4 * n, 4), v(c), v("hold" + s, 0, n), AL.is_lt)
+                    dg = wrap(v(tl, j, 4 * n, 4), n, "dgs" + s)
+                elif p in BOTH[t]:
+                    act(v("jr" + s, used, used + 16 * p), v(c, 0, 16 * p), AF.Sign, bias=v("hold" + s, 16 * p + 15, 16 * p + 16), scale=-1.0)
+                    act(v(tl, j, 64 * p, 4), v("jr" + s, used, used + 16 * p), AF.Sign, bias=1.0, acc=v("rs" + s, p, p + 1))
+                    used += 16 * p
+                elif p is not None:
+                    ts(v(tl, j, 64 * p, 4), v(c, 0, 16 * p), v("hold" + s, 16 * p + 15, 16 * p + 16), AL.is_le)
+                    act(v("jr" + s, used, used + 16 * p), v(tl, j, 64 * p, 4), AF.Copy, acc=v("rs" + s, p, p + 1))
+                    used += 16 * p
+            quant(v("tc%d%d" % (t, k)), v("ts%d%d" % (t, k)), v(tl))
+            mm(bank(6, 0, hi), v("bdqc"), v("bdqs"), v("tc%d%d" % (t, k)), v("ts%d%d" % (t, k)), k == len(tiles) - 1, k == 0)
+        tt(v("r1" + s, 0, K), dg, v("left" + s, 0, K), AL.add)
+        tt(v("r2" + s, 0, K), v("r1" + s, 0, K), v("rs" + s, 0, K), AL.add)
+        tt(v("colm" + s), bank(6, 0, n), v("mask", 0, n), AL.mult)
+        w = wrap(v("colm" + s), n, "cols" + s)
+        tt(v("r3" + s, 0, K), v("r2" + s, 0, K), w, AL.subtract)
+        ts(v("rk" + s, 0, K), v("r3" + s, 0, K), n - 16.0, AL.add)
+        scatter(v("ew" + s), v("rk" + s, 0, K), v("iota", 0, n))
+        tt(v("em" + s), v("ew" + s, 0, A), v("mask", 0, A), AL.mult)
+        w = wrap(v("em" + s), A, "ec" + s)
+        ts(v("es" + s, 0, 6), w, 256.0, AL.add)
+        far(v("el" + s, 0, 6), v("es" + s, 0, 6), "al" + s, False, FAR_LAT)
+
+        el = v("el" + s, 0, 6)
+        for b in range(4):
+            o = v("x" + s, 4 * n + b, 4 * m, 4)
+            if b % 2 == 0:
+                cp(o, at(v("dp%d%d" % (t, b)), el))
+            else:
+                act(o, at(v("dp%d%d" % (t, b)), el), AF.Copy)
+        quant(v("h%dc" % t), v("h%ds" % t), v("x" + s, 4 * (m - 128), 4 * m))
+        for b in range(4):
+            act(v("xh%d%d" % (t, b), n, m), v("x" + s, 4 * n + b, 4 * m, 4), AF.Copy, scale=0.5)
+            act(v("xo%d%d" % (b, t), n, m), v("x" + s, 4 * n + b, 4 * m, 4), AF.Copy, scale=0.5)
+        mm(bank(5, 0, 128), v("urc"), v("urs"), v("h%dc" % t), v("h%ds" % t))
+        z = bank(5, 128 - A, 128)
+        for i in range(4):
+            tt(v("d1" + s, i, SL, 4), z, v("sn" + s, i, SL, 4), AL.subtract)
+        act(v("gap" + s), v("d1" + s), AF.Abs)
+        for i in range(4):
+            tt(v("d2" + s, i, SL, 4), z, v("snm" + s, i, SL, 4), AL.subtract)
+        act(v("gaps" + s), at(v("d2" + s), v("so" + s)), AF.Abs)
+        tt(v("cost" + s), v("gap" + s), v("cn" + s), AL.max)
+        scan(v("f4" + s, 0, SL), v("r4"), v("cost" + s), HUGE, AL.add, AL.min)
+        for i in range(1, 4):
+            tt(v("keep" + s, i, SL, 4), v("f4" + s, i, SL, 4), v("f4" + s, i - 1, SL, 4), AL.is_equal)
+        scan(v("a4" + s), v("keep" + s), v("nu" + s), 0.0, AL.mult, AL.max)
+        tt(v("pm" + s), v("a4" + s, 3, SL, 4), v("mask", 0, A), AL.mult)
+        w = wrap(v("pm" + s), A, "ps" + s)
+        cp(v("pp" + s, 0, 6), w)
+        pw = "pw%d" % (t + 1)
+        ts(v(pw, K, K + 6), v("pp" + s, 0, 6), 511, AL.bitwise_and)
+        tt(v("price" + s), at(v("f4" + s, 0, SL), v("do" + s)), v("gaps" + s), AL.max)
+        scan(v("fs" + s, 0, SL), v("rr" + s, 15, 15 + SL), v("price" + s), HUGE, AL.add, AL.min)
+        tt(v("nf" + s), v("price" + s), v("fs" + s, 0, SL), AL.not_equal)
+        scan(v("as" + s, 0, SL), v("nf" + s), v("us" + s), 0.0, AL.mult, AL.max)
+        end = v("endo", 2 * t, 2 * t + 2)
+        tt(v("mv" + s), at(v("fs" + s), end), v("hold" + s, 15, 512, 16), AL.is_lt)
+        tt(v("dl" + s), at(v("as" + s), end), v("pw" + s), AL.subtract)
+        tt(v("dm" + s, 0, K), v("dl" + s, 0, K), v("mv" + s, 0, K), AL.mult)
+        tt(v(pw, 0, K), v("dm" + s, 0, K), v("pw" + s, 0, K), AL.add)
+        po = "po%d" % (t + 1)
+        cp(v(po, 0, K + 6), v(pw, 0, K + 6))
+
+        nx = "x%d" % (t + 1)
+        for h, (a, e) in enumerate(CHUNKS[t]):
+            for b in range(4):
+                tt(v("yt" + s, 4 * a + b, 4 * e, 4), at(v("xh%d%d" % (t, b)), v(po, a // 16, e // 16)), v("xo%d%d" % (b, t), a, e), AL.add)
+            quant(v("yq%dc" % t, a, e), v("yq%ds" % t, a, e), v("yt" + s, 4 * a, 4 * e))
+            for b in range(4):
+                k = 4 * h + b
+                mm(bank(k, 0, e - a), v("wqc", 128 * b, 128 * b + 128), v("wqs", 128 * b, 128 * b + 128),
+                   v("yq%dc" % t, a, e), v("yq%ds" % t, a, e))
+                act(v("rl%d%d" % (b, t), a, e), bank(k, 0, e - a), AF.Relu, scale=0.03125)
+                tt(v(nx, 4 * a + b, 4 * e, 4), v("rl%d%d" % (b, t), a, e), v("x" + s, 4 * a + b, 4 * e, 4), AL.add)
+            quant(v("q%dc" % (t + 1), a, e), v("q%ds" % (t + 1), a, e), v(nx, 4 * a, 4 * e))
+
+    act(v("opr"), at(v("iota"), v("po2")), AF.Identity, bias=256.0)
+    ob, oo, _c = PLACE["opr"]
+    for k in range(8):
+        dma("Y", lambda e, k=k: e.dma_start(T.op[k:k + 1, :], T[ob][16 * k:16 * k + 1, oo:oo + 512]), [v("opr")], [], "out")
+    for h, (a, e) in enumerate(CHUNKS[R - 1]):
+        dma("Y", lambda q, a=a, e=e: q.dma_start(T.oc[:, 4 * a:4 * e], ap(v("q2c", a, e)).bitcast(dt.uint8)), [v("q2c", a, e)], [], "out")
+        for k in range(4):
+            dma("Y" if h == 0 or k < 2 else "S",
+                lambda q, a=a, e=e, k=k: q.dma_start(T.osc[4 * k:4 * k + 4, a:e], T.q2s[32 * k:32 * k + 4, a:e]),
+                [v("q2s", a, e)], [], "out")
+        mm(bank(4 * h, 0, e - a), v("vqc"), v("vqs"), v("q2c", a, e), v("q2s", a, e))
+        act(v("ysb", a, e), bank(4 * h, 0, e - a), AF.Copy)
+        dma("S", lambda q, a=a, e=e: q.dma_start(T.y[:, a:e], ap(v("ysb", a, e))), [v("ysb", a, e)], [], "out")
+    return ops
+
+
+def depend(ops):
+    wr, rdrs = {}, {}
+    for i, o in enumerate(ops):
+        deps = set()
+        touched = []
+        for kind in ("r", "w"):
+            for x in o[kind]:
+                buf, off, _c = PLACE[x[0]]
+                if buf == "acc":
+                    cells = [("acc", x[1] // 512)]
+                else:
+                    cells = [(buf, off + j) for j in range(x[1], x[2], x[3])]
+                touched.append((kind, buf, cells))
+        for kind, buf, cells in touched:
+            for cell in cells:
+                if cell in wr:
+                    deps.add(wr[cell])
+                if kind == "w":
+                    deps.update(rdrs.get(cell, ()))
+                elif buf == "acc":
+                    deps.update(j for j in rdrs.get(cell, ()) if ops[j]["q"] != o["q"])
+        for kind, buf, cells in touched:
+            for cell in cells:
+                if kind == "w":
+                    wr[cell] = i
+                    rdrs[cell] = []
+        for kind, buf, cells in touched:
+            if kind == "r":
+                for cell in cells:
+                    if wr.get(cell) != i:
+                        rdrs.setdefault(cell, []).append(i)
+        deps.discard(i)
+        o["deps"] = sorted(deps)
+
+
+def place(ops, before, key):
+    n = len(ops)
+    busy = {q: [] for q in "VSTGY"}
+    start = [None] * n
+    back = before[1]
+    left = [len(b) for b in before[0]]
+    pool = [i for i in range(n) if left[i] == 0]
+    while pool:
+        i = min(pool, key=lambda j: key[j])
+        pool.remove(i)
+        o = ops[i]
+        if before[2]:
+            t = max([0.0] + [start[d] + ops[d]["cost"] + (ops[d]["lat"] if d in o["deps"] else 0) for d in before[0][i]])
+        else:
+            t = max([0.0] + [start[d] + ops[d]["cost"] + (o["lat"] if i in ops[d]["deps"] else 0) for d in before[0][i]])
+        row = busy[o["q"]]
+        k = 0
+        while k < len(row):
+            if row[k][1] > t:
+                if row[k][0] >= t + o["cost"]:
+                    break
+                t = row[k][1]
+            k += 1
+        row.insert(k, (t, t + o["cost"]))
+        start[i] = t
+        for j in back[i]:
+            left[j] -= 1
+            if left[j] == 0:
+                pool.append(j)
+    return start
+
+
+def replay(ops, order, lat):
+    free = {q: 0.0 for q in "VSTGY"}
+    fin = {}
+    for i in order:
+        o = ops[i]
+        start = max([free[o["q"]]] + [fin[d] for d in o["deps"]])
+        o["at"] = start
+        free[o["q"]] = start + o["cost"]
+        fin[i] = free[o["q"]] + max(lat, o["lat"])
+    return max(fin.values())
+
+
+EARLIER = [("pos0", "ew0"), ("pos1", "hold1"), ("endo", "so0"), ("sg0", "cnt"), ("ql11", "q1s"), ("ql12", "df1"), ("ql13", "cd1")]
+
+
+def plan(ops):
+    n = len(ops)
+    deps = [list(o["deps"]) for o in ops]
+    by = {}
+    for i in range(n):
+        by.setdefault(ops[i]["w"][-1][0] if ops[i]["w"] else "", []).append(i)
+    for x in ("sg0", "sg1", "cnt"):
+        for a, b in zip(by[x], by[x][1:]):
+            deps[b].append(a)
+    for x, y in EARLIER:
+        deps[by[y][0]].append(by[x][-1])
+    ahead = []
+    seen = set()
+
+    def visit(i):
+        if i not in seen:
+            seen.add(i)
+            for d in deps[i]:
+                visit(d)
+            ahead.append(i)
+
+    for i in range(n):
+        visit(i)
+    kids = [[] for _i in range(n)]
+    for i in range(n):
+        for d in deps[i]:
+            kids[d].append(i)
+    seed = [12345]
+
+    def draw(k):
+        seed[0] = (seed[0] * 1103515245 + 12345) % 2147483648
+        return (seed[0] >> 8) % k
+
+    key = [0.0] * n
+    for i in reversed(ahead):
+        key[i] = -ops[i]["cost"] - ops[i]["lat"] + min([key[k] for k in kids[i]] + [0.0])
+    best, order, kept = None, None, key
+    for r in range(TRIES):
+        start = place(ops, (deps, kids, True), key)
+        o = sorted(range(n), key=lambda i: (start[i], i))
+        s = replay(ops, o, LAT) + replay(ops, o, 2 * LAT)
+        if best is None or s <= best:
+            best, order, kept = s, o, start
+        if r % 4 == 3:
+            amp = (100, 400, 1500)[draw(3)]
+            start = [kept[i] + draw(amp) for i in range(n)]
+        late = place(ops, (kids, deps, False), [-(start[i] + ops[i]["cost"]) for i in range(n)])
+        key = [-(late[i] + ops[i]["cost"]) for i in range(n)]
+    return order
+
+
+PLAN = {}
+
+
+def rank_program(g, core, T, topo):
+    rank = T.rank_of(core)
+    if rank is None:
+        return
+    ops = build(g, T, topo, (core, T.cores[(rank + 1) % len(T.cores)]))
+    if not PLAN:
+        depend(ops)
+        PLAN["order"] = plan(ops)
+        PLAN["deps"] = [o["deps"] for o in ops]
+    queue = {"V": g.vector, "S": g.scalar, "T": g.tensor, "G": g, "Y": g.sync}
+    total = {}
+    for o in ops:
+        if o["sem"] is not None:
+            total[o["sem"]] = total.get(o["sem"], 0) + o["inc"]
+    done = {}
+    for i, o in enumerate(ops):
+        if o["sem"] is not None:
+            done[i] = (o["sem"], total[o["sem"]])
+    seen = {q: {} for q in queue}
+    sent = 0
+    for i in PLAN["order"]:
+        o = ops[i]
+        q = o["q"]
+        need = {}
+        for d in PLAN["deps"][i]:
+            sem, val = done[d]
+            need[sem] = max(need.get(sem, 0), val)
+        for sem in need:
+            if seen[q].get(sem, 0) < need[sem]:
+                queue[q].wait_ge(T.sem[sem], need[sem])
+                seen[q][sem] = need[sem]
+        ins = o["fn"]()
+        if o["sem"] is None:
+            sem = "c" + q
+            total[sem] = total.get(sem, 0) + 1
+            ins.then_inc(T.sem[sem], 1)
+            done[i] = (sem, total[sem])
+        elif o["sem"] in FAR:
+            sent += o["inc"]
+        else:
+            ins.then_inc(T.sem[o["sem"]], 16)
+    total["sent"] = sent
+    for sem in total:
+        if seen["G"].get(sem, 0) < total[sem]:
+            g.wait_ge(T.sem[sem], total[sem])

@@ -8,9 +8,7 @@ BIG, HUGE = 1e29, 5e29
 RADIX = [[3, 3, 4, 0], [3, 3, 3, 4, 4]]
 STEP = 32
 BOTH = [[], [22, 18, 14]]
-CHUNKS = [[(0, 192), (192, 416)], [(0, 320), (320, 512)]]
-LAT, DMA_LAT, FAR_LAT = 130, 2600, 3000
-TRIES = 600
+CHUNKS = [[(0, 192), (192, 416)], [(0, 256), (256, 512)]]
 
 BYTES = {"float32": 4, "int32": 4, "bfloat16": 2, "uint16": 2, "uint8": 1, "float8_e4m3fn_x4": 4}
 ARENA = {}
@@ -151,10 +149,6 @@ def count(x):
     return len(range(x[1], x[2], x[3]))
 
 
-def wide(x):
-    return 4 if x[0] == "acc" else BYTES[ARENA[PLACE[x[0]][0]][0]]
-
-
 def bank(k, a, b, s=1):
     return ("acc", 512 * k + a, 512 * k + b, s)
 
@@ -184,45 +178,36 @@ def build(g, T, topo, dst):
     def sc(x):
         return ap(x) if isinstance(x, tuple) else x
 
-    def add(q, fn, reads, writes, cost, sem=None, inc=1, lat=LAT):
-        ops.append({"q": q, "fn": fn, "r": reads, "w": writes, "cost": cost, "sem": sem, "inc": inc, "lat": lat})
+    def add(q, fn, reads, writes, sem=None, inc=1):
+        ops.append({"q": q, "fn": fn, "r": reads, "w": writes, "sem": sem, "inc": inc})
 
     def at(win, off):
         return ("@", win, off)
 
-    def vcost(out, ins, two):
-        n = count(out)
-        if ins[0][0] == "@":
-            return 60 + 1.56 * n
-        if two:
-            return max(64, n * (1 if any(x[0] == "acc" for x in ins) else 2))
-        return max(64, n * (0.5 if all(wide(x) == 2 for x in ins + [out]) else 1))
-
     def tt(out, a, b, op):
-        add("V", lambda: g.vector.tensor_tensor(ap(out), src(a), ap(b), op), rd(a) + [b], [out], vcost(out, [a, b], True))
+        add("V", lambda: g.vector.tensor_tensor(ap(out), src(a), ap(b), op), rd(a) + [b], [out])
 
     def ts(out, a, s1, op0, s2=None, op1=None):
         if op1 is None:
             fn = lambda: g.vector.tensor_scalar(ap(out), src(a), sc(s1), None, op0)
         else:
             fn = lambda: g.vector.tensor_scalar(ap(out), src(a), sc(s1), sc(s2), op0, op1)
-        add("V", fn, rd(a) + rd(s1) + rd(s2), [out], vcost(out, [a], False))
+        add("V", fn, rd(a) + rd(s1) + rd(s2), [out])
 
     def cp(out, a):
-        add("V", lambda: g.vector.tensor_copy(ap(out), src(a)), rd(a), [out], vcost(out, [a], False))
+        add("V", lambda: g.vector.tensor_copy(ap(out), src(a)), rd(a), [out])
 
     def scatter(win, off, a):
-        add("V", lambda: g.vector.tensor_copy(ap(win).indirect(ap(off)), ap(a)), [a, off], [win], 60 + 3.8 * count(a))
+        add("V", lambda: g.vector.tensor_copy(ap(win).indirect(ap(off)), ap(a)), [a, off], [win])
 
     def scan(out, d0, d1, init, op0, op1):
-        add("V", lambda: g.vector.tensor_tensor_scan(ap(out), ap(d0), ap(d1), init, op0, op1), [d0, d1], [out],
-            vcost(out, [d0, d1], False))
+        add("V", lambda: g.vector.tensor_tensor_scan(ap(out), ap(d0), ap(d1), sc(init), op0, op1), [d0, d1] + rd(init), [out])
 
     def fill(out, c):
-        add("V", lambda: g.vector.memset(ap(out), c), [], [out], max(64, count(out) * wide(out) / 4))
+        add("V", lambda: g.vector.memset(ap(out), c), [], [out])
 
     def quant(qc, qs, x):
-        add("V", lambda: g.vector.quantize_mx(ap(qc), ap(qs), ap(x)), [x], [qc, qs], 15 + 0.27 * count(x))
+        add("V", lambda: g.vector.quantize_mx(ap(qc), ap(qs), ap(x)), [x], [qc, qs])
 
     def act(out, a, f, bias=None, scale=None, acc=None):
         kw = {}
@@ -232,43 +217,54 @@ def build(g, T, topo, dst):
             kw["scale"] = scale
         if acc is not None:
             kw["accum_out"] = acc
-        n = count(out)
-        cost = (80 + 1.56 * n if a[0] == "@" else 60 + n) + (25 if acc else 0)
         add("S", lambda: g.scalar.activation(ap(out), src(a), f, **{k: sc(x) for k, x in kw.items()}),
-            rd(a) + rd(bias), [out] + rd(acc), cost)
+            rd(a) + rd(bias), [out] + rd(acc))
 
     def iota(out, pat, base, cm):
         if ARENA[PLACE[out[0]][0]][0] == I:
             fn = lambda: g.iota(ap(out), pat, base, cm)
         else:
             fn = lambda: g.iota(ap(out), pat, base, cm, allow_small_or_imprecise_dtypes=True)
-        add("G", fn, [], [out], 160 + 2 * count(out))
+        add("G", fn, [], [out])
 
     def zero(out):
         iota(out, [[0, count(out)]], 0, 0)
 
     def mm(out, wc, ws, xc, xs, start=True, stop=True):
-        add("T", lambda: g.tensor.matmul_mx(ap(out), ap(wc), ap(ws), ap(xc), ap(xs), start, stop), [wc, ws, xc, xs], [out],
-            (count(out) + 16) * 1.2)
+        add("T", lambda: g.tensor.matmul_mx(ap(out), ap(wc), ap(ws), ap(xc), ap(xs), start, stop), [wc, ws, xc, xs], [out])
 
-    def dma(q, fn, reads, writes, sem, lat=DMA_LAT):
+    def dma(q, fn, reads, writes, sem):
         e = g.sync if q == "Y" else g.scalar
-        add(q, lambda: fn(e), reads, writes, 80, sem, 16, lat)
+        add(q, lambda: fn(e), reads, writes, sem, 16)
 
-    def far(out, a, sem, codes, lat):
+    def far(out, a, sem, codes):
         if codes:
             fn = lambda: g.remote_dma(ap(out).bitcast(dt.uint8), ap(a).bitcast(dt.uint8), T.sem[sem], T.sem.sent, pid, rid, far_mask)
         else:
             fn = lambda: g.remote_dma(ap(out), ap(a), T.sem[sem], T.sem.sent, pid, rid, far_mask)
-        add("G", fn, [a], [out], 600, sem, far_n, lat)
+        add("G", fn, [a], [out], sem, far_n)
 
     def wrap(spread, n, tmp):
         scan(v(tmp, 0, n), v("rst", 0, n), spread, 0.0, AL.mult, AL.add)
         return v(tmp, 15, n, 16)
 
+    def part(x, a, b):
+        return (x[0], x[1] + a * x[3], min(x[2], x[1] + b * x[3]), x[3])
+
+    def cuts(n):
+        h = (n // 32 + 1) // 2 * 32
+        return ((0, h), (h, n))
+
+    def masked(out, tmp, a, n):
+        for lo, hi in cuts(n):
+            tt(v(tmp, lo, hi), part(a, lo, hi), v("mask", lo, hi), AL.mult)
+        for lo, hi in cuts(n):
+            scan(v(out, lo, hi), v("rst", lo, hi), v(tmp, lo, hi), 0.0, AL.mult, AL.add)
+        return v(out, 15, n, 16)
+
     dma("S", lambda e: e.dma_start(ap(v("pw0", 0, 20)), T.pa[:]), [], [v("pw0", 0, 20)], "lpa")
     dma("Y", lambda e: e.dma_start(ap(v("ut")), T.u[:]), [], [v("ut")], "lu")
-    dma("Y", lambda e: e.dma_start(ap(v("x0", 0, 4 * C)), T.x[:]), [], [v("x0", 0, 4 * C)], "lx", DMA_LAT + 600)
+    dma("Y", lambda e: e.dma_start(ap(v("x0", 0, 4 * C)), T.x[:]), [], [v("x0", 0, 4 * C)], "lx")
     dma("S", lambda e: e.dma_start(ap(v("nri")), T.nr[:]), [], [v("nri")], "lnr")
     dma("Y", lambda e: e.dma_start(ap(v("wqc")).bitcast(dt.uint8), T.wc[:]), [], [v("wqc")], "lwc")
     dma("Y", lambda e: e.dma_start(ap(v("wqs")), T.ws[:]), [], [v("wqs")], "lws")
@@ -296,7 +292,7 @@ def build(g, T, topo, dst):
     cp(v("upo"), v("upi"))
     for b in range(4):
         add("G", lambda b=b: g.affine_select(ap(v("et%d" % b)), ap(v("ones")), [[-1, 512]], AL.is_equal, 0.0, b, 4),
-            [v("ones")], [v("et%d" % b)], 1230)
+            [v("ones")], [v("et%d" % b)])
         quant(v("eqc", 128 * b, 128 * b + 128), v("eqs", 128 * b, 128 * b + 128), v("et%d" % b))
     ts(v("bd"), v("blk"), v("gf"), AL.is_equal)
     quant(v("bdqc"), v("bdqs"), v("bd"))
@@ -304,9 +300,9 @@ def build(g, T, topo, dst):
         ts(v("slw", 24 * t, 24 * t + 24), v("plw", 0, 24), v("rf"), AL.add, -256.0, AL.add)
     quant(v("uqc"), v("uqs"), v("ut"))
     add("V", lambda: g.vector.tensor_copy(ap(v("urc")).bitcast(dt.uint32), ap(v("uqc")).bitcast(dt.uint32).indirect(ap(v("upo")))),
-        [v("uqc"), v("upo")], [v("urc")], 260)
+        [v("uqc"), v("upo")], [v("urc")])
     add("S", lambda: g.scalar.activation(ap(v("urs")), ap(v("uqs")).indirect(ap(v("upo"))), AF.Copy),
-        [v("uqs"), v("upo")], [v("urs")], 280)
+        [v("uqs"), v("upo")], [v("urs")])
     quant(v("vqc"), v("vqs"), v("vt"))
 
     cp(v("nro"), v("nri"))
@@ -323,12 +319,13 @@ def build(g, T, topo, dst):
             col = 4 * (i // 2) + 2 * t + i % 2
             act(v("jc", SL * i, SL * i + SL), v("key", SL * t, SL * t + SL), AF.Sign, bias=v("bkt", i, i + 1),
                 acc=v("cnt", col, col + 1))
-    ts(v("e1"), v("cnt", 0, 4), 0.5, AL.mult, 191.0, AL.add)
-    tt(v("em"), v("cnt", 0, 4), v("cnt", 4, 8), AL.is_equal)
-    tt(v("e2"), v("dum"), v("e1"), AL.subtract)
-    tt(v("e3"), v("e2"), v("em"), AL.mult)
-    tt(v("e4"), v("e3"), v("e1"), AL.add)
-    cp(v("endo"), v("e4"))
+        a, e = 2 * t, 2 * t + 2
+        ts(v("e1", a, e), v("cnt", a, e), 0.5, AL.mult, 191.0, AL.add)
+        tt(v("em", a, e), v("cnt", a, e), v("cnt", 4 + a, 4 + e), AL.is_equal)
+        tt(v("e2", a, e), v("dum", a, e), v("e1", a, e), AL.subtract)
+        tt(v("e3", a, e), v("e2", a, e), v("em", a, e), AL.mult)
+        tt(v("e4", a, e), v("e3", a, e), v("e1", a, e), AL.add)
+        cp(v("endo", a, e), v("e4", a, e))
     for t in range(R):
         act(v("near%d" % t), at(v("iota"), v("nro", 24 * t, 24 * t + 24)), AF.Identity, bias=256.0)
         for i in range(4):
@@ -348,8 +345,7 @@ def build(g, T, topo, dst):
                 bias=v("nkey", 24 * t + c, 24 * t + c + 1), acc=v("sg" + s, c, c + 1))
         ts(v("pos" + s), v("sg" + s), 383.0, AL.add, 0.5, AL.mult)
         scatter(v("sw" + s), v("pos" + s), v("iota", 0, SL))
-        tt(v("swm" + s), v("sw" + s), v("mask", 0, SL), AL.mult)
-        w = wrap(v("swm" + s), SL, "sws" + s)
+        w = masked("sws" + s, "swm" + s, v("sw" + s), SL)
         ts(v("so" + s), w, 256.0, AL.add)
         ts(v("si" + s), w, 256.0, AL.add)
         ts(v("sh" + s), v("si" + s), 2, AL.arith_shift_right)
@@ -371,14 +367,17 @@ def build(g, T, topo, dst):
         qc, qs = v("q%dc" % t), v("q%ds" % t)
         if t == 0:
             quant(qc, qs, v("x0", 0, 4 * n))
-        far(v("l%dc" % t), qc, "ac" + s, True, FAR_LAT + 1500)
-        far(v("l%ds" % t), qs, "ac" + s, False, FAR_LAT + 1500)
+        far(v("l%dc" % t), qc, "ac" + s, True)
+        far(v("l%ds" % t), qs, "ac" + s, False)
         mm(bank(4, 0, n), v("urc"), v("urs"), qc, qs)
+        mm(bank(7, 0, n), v("urc"), v("urs"), qc, qs)
         cp(v("s" + s), bank(4, 0, n))
-        act(v("sp" + s), at(v("s" + s), v("po" + s, 0, K)), AF.Copy)
-        tt(v("df" + s), bank(4, 0, n), v("sp" + s), AL.subtract)
-        act(v("ca" + s), v("df" + s), AF.Abs)
-        act(v("ce" + s), v("df" + s), AF.Abs)
+        act(v("sp" + s), bank(7, 0, n), AF.Copy)
+        for lo, hi in cuts(n):
+            tt(v("df" + s, lo, hi), at(v("s" + s), v("po" + s, lo // 16, hi // 16)), v("sp" + s, lo, hi), AL.subtract)
+        for lo, hi in cuts(n):
+            act(v("ca" + s, lo, hi), v("df" + s, lo, hi), AF.Abs)
+            act(v("ce" + s, lo, hi), v("df" + s, lo, hi), AF.Abs)
         tt(v("sm" + s), bank(4, 0, n), v("offd", 0, n), AL.add)
         act(v("sn" + s), at(v("s" + s), nro), AF.Copy)
         act(v("snm" + s), at(v("sm" + s), nro), AF.Copy)
@@ -418,8 +417,7 @@ def build(g, T, topo, dst):
         c = cs[0]
         act(v("cn" + s), at(v(c), nro), AF.Copy)
 
-        tt(v("cm" + s), v(c), v("mask", 0, n), AL.mult)
-        scan(v("hold" + s, 0, n), v("rst", 0, n), v("cm" + s), 0.0, AL.mult, AL.add)
+        masked("hold" + s, "cm" + s, v(c), n)
         used = 0
         for k in range(len(tiles) - 1, -1, -1):
             tl = "tl%d%d" % (t, k)
@@ -441,15 +439,14 @@ def build(g, T, topo, dst):
             mm(bank(6, 0, hi), v("bdqc"), v("bdqs"), v("tc%d%d" % (t, k)), v("ts%d%d" % (t, k)), k == len(tiles) - 1, k == 0)
         tt(v("r1" + s, 0, K), dg, v("left" + s, 0, K), AL.add)
         tt(v("r2" + s, 0, K), v("r1" + s, 0, K), v("rs" + s, 0, K), AL.add)
-        tt(v("colm" + s), bank(6, 0, n), v("mask", 0, n), AL.mult)
-        w = wrap(v("colm" + s), n, "cols" + s)
+        w = masked("cols" + s, "colm" + s, bank(6, 0, n), n)
         tt(v("r3" + s, 0, K), v("r2" + s, 0, K), w, AL.subtract)
         ts(v("rk" + s, 0, K), v("r3" + s, 0, K), n - 16.0, AL.add)
         scatter(v("ew" + s), v("rk" + s, 0, K), v("iota", 0, n))
         tt(v("em" + s), v("ew" + s, 0, A), v("mask", 0, A), AL.mult)
         w = wrap(v("em" + s), A, "ec" + s)
         ts(v("es" + s, 0, 6), w, 256.0, AL.add)
-        far(v("el" + s, 0, 6), v("es" + s, 0, 6), "al" + s, False, FAR_LAT)
+        far(v("el" + s, 0, 6), v("es" + s, 0, 6), "al" + s, False)
 
         el = v("el" + s, 0, 6)
         for b in range(4):
@@ -466,11 +463,12 @@ def build(g, T, topo, dst):
         z = bank(5, 128 - A, 128)
         for i in range(4):
             tt(v("d1" + s, i, SL, 4), z, v("sn" + s, i, SL, 4), AL.subtract)
-        act(v("gap" + s), v("d1" + s), AF.Abs)
+            act(v("gap" + s, i, SL, 4), v("d1" + s, i, SL, 4), AF.Abs)
         for i in range(4):
             tt(v("d2" + s, i, SL, 4), z, v("snm" + s, i, SL, 4), AL.subtract)
         act(v("gaps" + s), at(v("d2" + s), v("so" + s)), AF.Abs)
-        tt(v("cost" + s), v("gap" + s), v("cn" + s), AL.max)
+        for i in range(4):
+            tt(v("cost" + s, i, SL, 4), v("gap" + s, i, SL, 4), v("cn" + s, i, SL, 4), AL.max)
         scan(v("f4" + s, 0, SL), v("r4"), v("cost" + s), HUGE, AL.add, AL.min)
         for i in range(1, 4):
             tt(v("keep" + s, i, SL, 4), v("f4" + s, i, SL, 4), v("f4" + s, i - 1, SL, 4), AL.is_equal)
@@ -480,10 +478,13 @@ def build(g, T, topo, dst):
         cp(v("pp" + s, 0, 6), w)
         pw = "pw%d" % (t + 1)
         ts(v(pw, K, K + 6), v("pp" + s, 0, 6), 511, AL.bitwise_and)
-        tt(v("price" + s), at(v("f4" + s, 0, SL), v("do" + s)), v("gaps" + s), AL.max)
-        scan(v("fs" + s, 0, SL), v("rr" + s, 15, 15 + SL), v("price" + s), HUGE, AL.add, AL.min)
-        tt(v("nf" + s), v("price" + s), v("fs" + s, 0, SL), AL.not_equal)
-        scan(v("as" + s, 0, SL), v("nf" + s), v("us" + s), 0.0, AL.mult, AL.max)
+        for lo, hi in cuts(SL):
+            tt(v("price" + s, lo, hi), at(v("f4" + s, 0, SL), v("do" + s, lo // 16, hi // 16)), v("gaps" + s, lo, hi), AL.max)
+        for lo, hi in cuts(SL):
+            scan(v("fs" + s, lo, hi), v("rr" + s, 15 + lo, 15 + hi), v("price" + s, lo, hi), v("fs" + s, lo - 1, lo) if lo else HUGE,
+                 AL.add, AL.min)
+            tt(v("nf" + s, lo, hi), v("price" + s, lo, hi), v("fs" + s, lo, hi), AL.not_equal)
+            scan(v("as" + s, lo, hi), v("nf" + s, lo, hi), v("us" + s, lo, hi), v("as" + s, lo - 1, lo) if lo else 0.0, AL.mult, AL.max)
         end = v("endo", 2 * t, 2 * t + 2)
         tt(v("mv" + s), at(v("fs" + s), end), v("hold" + s, 15, 512, 16), AL.is_lt)
         tt(v("dl" + s), at(v("as" + s), end), v("pw" + s), AL.subtract)
@@ -556,103 +557,8 @@ def depend(ops):
         o["deps"] = sorted(deps)
 
 
-def place(ops, before, key):
-    n = len(ops)
-    busy = {q: [] for q in "VSTGY"}
-    start = [None] * n
-    back = before[1]
-    left = [len(b) for b in before[0]]
-    pool = [i for i in range(n) if left[i] == 0]
-    while pool:
-        i = min(pool, key=lambda j: key[j])
-        pool.remove(i)
-        o = ops[i]
-        if before[2]:
-            t = max([0.0] + [start[d] + ops[d]["cost"] + (ops[d]["lat"] if d in o["deps"] else 0) for d in before[0][i]])
-        else:
-            t = max([0.0] + [start[d] + ops[d]["cost"] + (o["lat"] if i in ops[d]["deps"] else 0) for d in before[0][i]])
-        row = busy[o["q"]]
-        k = 0
-        while k < len(row):
-            if row[k][1] > t:
-                if row[k][0] >= t + o["cost"]:
-                    break
-                t = row[k][1]
-            k += 1
-        row.insert(k, (t, t + o["cost"]))
-        start[i] = t
-        for j in back[i]:
-            left[j] -= 1
-            if left[j] == 0:
-                pool.append(j)
-    return start
-
-
-def replay(ops, order, lat):
-    free = {q: 0.0 for q in "VSTGY"}
-    fin = {}
-    for i in order:
-        o = ops[i]
-        start = max([free[o["q"]]] + [fin[d] for d in o["deps"]])
-        o["at"] = start
-        free[o["q"]] = start + o["cost"]
-        fin[i] = free[o["q"]] + max(lat, o["lat"])
-    return max(fin.values())
-
-
-EARLIER = [("pos0", "ew0"), ("pos1", "hold1"), ("endo", "so0"), ("sg0", "cnt"), ("ql11", "q1s"), ("ql12", "df1"), ("ql13", "cd1")]
-
-
-def plan(ops):
-    n = len(ops)
-    deps = [list(o["deps"]) for o in ops]
-    by = {}
-    for i in range(n):
-        by.setdefault(ops[i]["w"][-1][0] if ops[i]["w"] else "", []).append(i)
-    for x in ("sg0", "sg1", "cnt"):
-        for a, b in zip(by[x], by[x][1:]):
-            deps[b].append(a)
-    for x, y in EARLIER:
-        deps[by[y][0]].append(by[x][-1])
-    ahead = []
-    seen = set()
-
-    def visit(i):
-        if i not in seen:
-            seen.add(i)
-            for d in deps[i]:
-                visit(d)
-            ahead.append(i)
-
-    for i in range(n):
-        visit(i)
-    kids = [[] for _i in range(n)]
-    for i in range(n):
-        for d in deps[i]:
-            kids[d].append(i)
-    seed = [12345]
-
-    def draw(k):
-        seed[0] = (seed[0] * 1103515245 + 12345) % 2147483648
-        return (seed[0] >> 8) % k
-
-    key = [0.0] * n
-    for i in reversed(ahead):
-        key[i] = -ops[i]["cost"] - ops[i]["lat"] + min([key[k] for k in kids[i]] + [0.0])
-    best, order, kept = None, None, key
-    for r in range(TRIES):
-        start = place(ops, (deps, kids, True), key)
-        o = sorted(range(n), key=lambda i: (start[i], i))
-        s = replay(ops, o, LAT) + replay(ops, o, 2 * LAT)
-        if best is None or s <= best:
-            best, order, kept = s, o, start
-        if r % 4 == 3:
-            amp = (100, 400, 1500)[draw(3)]
-            start = [kept[i] + draw(amp) for i in range(n)]
-        late = place(ops, (kids, deps, False), [-(start[i] + ops[i]["cost"]) for i in range(n)])
-        key = [-(late[i] + ops[i]["cost"]) for i in range(n)]
-    return order
-
+ORDER = [
+    0,1,9,25,394,2,3,123,6,7,14,4,5,11,18,10,15,16,19,26,17,38,37,399,128,13,85,39,166,43,8,46,40,47,134,41,44,167,138,12,137,33,48,140,42,21,171,139,62,49,141,89,27,35,86,142,20,88,51,50,168,29,143,144,36,146,169,145,170,91,172,83,174,31,173,90,175,87,23,22,179,176,93,180,121,178,28,177,181,92,129,24,182,147,32,30,187,34,132,183,188,133,94,184,398,95,126,189,96,124,185,392,98,190,99,186,191,97,192,130,193,102,194,400,195,201,105,196,101,197,203,198,402,245,108,249,251,199,235,239,107,202,135,247,231,250,204,252,406,103,237,241,205,104,127,136,211,240,236,215,84,100,209,131,219,248,207,212,125,217,106,213,210,221,396,214,227,208,229,223,218,225,224,403,243,238,233,228,45,230,234,401,232,244,226,253,206,216,254,405,255,220,257,258,242,404,160,259,222,260,156,246,397,149,256,152,395,261,262,164,109,263,52,73,110,264,165,265,266,157,111,267,148,161,53,55,56,112,54,113,153,114,57,115,58,158,117,59,116,118,60,119,61,159,271,270,269,268,200,272,122,281,74,282,284,278,286,76,288,290,283,291,292,287,295,289,285,297,162,298,296,274,293,163,77,299,294,300,301,150,308,120,309,151,310,302,154,311,75,155,78,313,303,314,357,312,362,304,315,316,280,305,317,275,306,276,318,273,307,319,279,320,277,339,438,340,81,342,80,79,439,321,341,360,322,343,443,440,344,350,82,345,347,323,351,353,324,358,441,325,348,352,359,332,329,442,349,354,326,335,330,346,333,327,331,446,334,328,336,355,361,337,364,356,365,338,447,408,410,363,450,409,407,448,449,411,412,454,413,414,415,455,416,418,417,456,458,444,367,457,445,366,419,451,436,462,452,424,463,428,453,432,464,459,369,460,370,371,461,368,465,467,466,374,468,376,372,469,373,470,375,471,378,472,377,380,473,63,474,379,64,381,476,65,477,429,478,479,524,486,500,510,496,490,480,497,501,494,511,504,482,495,514,487,484,483,492,506,515,488,491,502,493,489,512,498,525,485,526,516,499,508,505,520,527,509,530,503,518,522,513,519,532,536,534,528,521,540,538,537,529,517,542,67,544,533,539,481,535,69,545,531,546,543,523,548,541,549,507,550,551,426,547,552,66,553,427,554,421,425,420,68,555,70,437,556,71,557,382,558,430,475,431,434,72,384,433,435,383,422,386,385,393,388,423,387,389,390,561,562,559,560,571,563,570,566,572,568,565,575,564,579,577,576,573,582,578,581,574,583,587,580,588,569,567,586,589,584,590,585,593,591,391,599,600,601,592,602,604,603,605,594,606,595,608,607,596,609,597,610,598,611,613,648,612,614,655,656,654,652,649,615,650,651,653,631,616,630,617,626,632,618,623,627,633,620,624,619,621,634,628,638,635,625,639,641,636,622,644,642,640,645,637,643,646,629,647,657,662,658,659,666,669,670,660,668,665,663,667,661,671,664,672]
 
 PLAN = {}
 
@@ -664,7 +570,6 @@ def rank_program(g, core, T, topo):
     ops = build(g, T, topo, (core, T.cores[(rank + 1) % len(T.cores)]))
     if not PLAN:
         depend(ops)
-        PLAN["order"] = plan(ops)
         PLAN["deps"] = [o["deps"] for o in ops]
     queue = {"V": g.vector, "S": g.scalar, "T": g.tensor, "G": g, "Y": g.sync}
     total = {}
@@ -677,7 +582,7 @@ def rank_program(g, core, T, topo):
             done[i] = (o["sem"], total[o["sem"]])
     seen = {q: {} for q in queue}
     sent = 0
-    for i in PLAN["order"]:
+    for i in ORDER:
         o = ops[i]
         q = o["q"]
         need = {}

from concourse.mybir import dt, AluOpType, ActivationFunctionType

AL = AluOpType
AF = ActivationFunctionType
C, A, R = 320, 96, 2
SL = 4 * A
BIG, HUGE = 1e29, 5e29
RADIX = [[3, 3, 4, 0], [3, 3, 3, 4, 4]]
STEP = 32
BOTH = [[], [22, 18, 14]]
CHUNKS = [[(0, 192), (192, 416)], [(0, 256), (256, 512)]]

BYTES = {"float32": 4, "int32": 4, "bfloat16": 2, "uint16": 2, "uint8": 1, "float8_e4m3fn_x4": 4}
ARENA = {}
PLACE = {}


def region(name, buf, dtype, cols):
    if buf not in ARENA:
        ARENA[buf] = [dtype, 0]
    al = 32 // BYTES[dtype]
    off = (ARENA[buf][1] + al - 1) // al * al
    PLACE[name] = (buf, off, cols)
    ARENA[buf][1] = off + cols


def shared(name, t, buf, dtype, cols):
    if t == R - 1:
        region(name + str(t), buf, dtype, cols)
    else:
        last = PLACE[name + str(R - 1)]
        PLACE[name + str(t)] = (last[0], last[1], cols)


def own(name, dtype, cols):
    region(name, name, dtype, cols)


def pair(name, cols):
    own(name + "c", "float8_e4m3fn_x4", cols)
    own(name + "s", "uint8", cols)


def planes_of(n):
    pl = list(range(1, n // 16)) + ["D"]
    pl = [None] * (-len(pl) % 4) + pl
    return [pl[i:i + 4] for i in range(0, len(pl), 4)]


def width(p, n):
    return 0 if p is None else n if p == "D" else 16 * p


F, B, I, U = "float32", "bfloat16", "int32", "uint16"
for _n, _c in (("ones", 512), ("iota", 512), ("mod16", 512), ("mask", 512), ("rst", 512), ("offd", 512), ("r4", SL),
               ("blk", 512), ("hugeb", 32)):
    region(_n, "kb", B, _c)
for _n, _c in (("rf", 1), ("gf", 1), ("hit", 512), ("cb", 4), ("bkt", 4), ("dum", 4), ("slw", 48),
               ("plw", 32), ("left0", 32), ("left1", 32)):
    region(_n, "kf", F, _c)
for _n, _c in (("pi", 1), ("ri", 1), ("gi", 1), ("upi", 8)):
    region(_n, "ki", I, _c)
own("upo", U, 8)
for _b in range(4):
    region("et%d" % _b, "kt", B, 512)
region("bd", "kt", B, 512)
pair("eq", 512)
pair("bdq", 128)
own("ut", B, 512)
own("vt", B, 512)
pair("uq", 128)
pair("ur", 128)
pair("vq", 128)
pair("wq", 512)
own("pw0", I, 32)
own("nri", I, 48)
region("nro", "ou", U, 48)
region("endo", "ou", U, 4)
for _n, _c in (("key", 2 * SL), ("nu0", SL), ("nu1", SL), ("near0", SL), ("near1", SL), ("nkey", 48), ("hi2", 48), ("cnt", 8),
               ("e1", 4), ("e2", 4), ("e3", 4), ("e4", 4), ("em", 4), ("opr", 512)):
    region(_n, "xf", F, _c)
region("hi1", "xi", I, 48)
own("x2", B, 2048)
pair("q2", 512)
own("ysb", F, 512)
for _t in range(R - 1, -1, -1):
    _n = C + A * _t
    _s = str(_t)
    own("x" + _s, B, 4 * (_n + A))
    pair("q" + _s, _n)
    pair("l" + _s, _n)
    pair("h" + _s, 128)
    pair("yq" + _s, _n + A)
    own("el" + _s, U, 8)
    own("es" + _s, U, 8)
    shared("yt", _t, "yt", B, 4 * (_n + A))
    region("pw" + str(_t + 1), "xi", I, 32)
    region("po" + _s, "ou", U, 32)
    for _b in range(4):
        region("xh%d%d" % (_t, _b), "xh" + _s, B, _n + A)
        shared("xo%d" % _b, _t, "xo", B, _n + A)
        region("dp%d%d" % (_t, _b), "dp" + _s, B, _n)
        shared("rl%d" % _b, _t, "rl", F, _n + A)
    for _x, _c in (("s", _n), ("sp", _n), ("ce", _n), ("sm", _n), ("df", _n), ("ca", _n), ("cc", _n), ("cd", _n), ("cm", _n),
                   ("hold", 512), ("sn", SL), ("snm", SL), ("cn", SL), ("d1", SL), ("d2", SL), ("gap", SL), ("gaps", SL),
                   ("cost", SL), ("f4", SL + 8), ("price", SL), ("fs", 424)):
        if _x in ("d1", "d2", "gap", "gaps", "cost", "price", "df", "cm", "sm", "cc", "cd", "sp", "ce"):
            shared(_x, _t, "sc", F, _c)
        else:
            region(_x + _s, "sc", F, _c)
    for _x, _c in (("rs", 32), ("colm", _n), ("cols", _n), ("r1", 32), ("r2", 32), ("r3", 32), ("sg", 24), ("a4", SL), ("pm", A),
                   ("ps", A), ("us", SL), ("as", 424), ("mv", 32), ("dl", 32), ("dm", 32)):
        region(_x + _s, "xf", F, _c)
    for _x, _c in (("wa", _n), ("wb", _n), ("wc", _n), ("gm", _n), ("gs", _n), ("dgs", _n), ("ew", _n), ("em", A), ("ec", A),
                   ("sw", SL), ("swm", SL), ("sws", SL), ("keep", SL), ("nf", SL), ("rr", 448)):
        region(_x + _s, "xb", B, _c)
    for _x, _c in (("si", 24), ("sh", 24), ("pp", 8)):
        region(_x + _s, "xi", I, _c)
    for _x, _c in (("rk", 32), ("pos", 24), ("so", 24), ("do", 24)):
        region(_x + _s, "ou", U, _c)
    for _k in range(1, len(RADIX[_t])):
        region("ql%d%d" % (_t, _k), "ou", U, 32)
    for _m, _pl in enumerate(planes_of(_n)):
        _w = max(128, width(_pl[3], _n))
        region("tl%d%d" % (_t, _m), "tl" + _s, B, 4 * _w)
        region("tc%d%d" % (_t, _m), "tc" + _s, "float8_e4m3fn_x4", _w)
        region("ts%d%d" % (_t, _m), "ts" + _s, "uint8", _w)
    shared("jr", _t, "jrow", B, 8 * (_n // 16) * (_n // 16))
    shared("js", _t, "junk", B, 6 * SL)
region("po2", "ou", U, 32)
region("jc", "junk", B, 4 * SL)

SCRATCH = {}
for _k, _v in ARENA.items():
    SCRATCH[_k] = ("sbuf", [128, _v[1] + _v[1] % 2], _v[0])
SCRATCH["acc"] = ("psum", [128, 4096], "float32")
PLACE["acc"] = ("acc", 0, 4096)

LOADS = ["lx", "lu", "lpa", "lnr", "lwc", "lws", "lv"]
FAR = ["ac0", "ac1", "al0", "al1"]
SEMAPHORES = ["cV", "cS", "cT", "cG", "out", "sent", "xo0", "xo1"] + LOADS + FAR


def v(name, a=0, b=None, s=1):
    return (name, a, PLACE[name][2] if b is None else b, s)


def count(x):
    return len(range(x[1], x[2], x[3]))


def bank(k, a, b, s=1):
    return ("acc", 512 * k + a, 512 * k + b, s)


def build(g, T, topo, dst):
    ops = []
    rid, pid, _se = topo.addr(dst[1])
    far_mask = topo.mask(dst[0], dst[1])
    far_n = len(topo.engines(dst[0], dst[1]))

    def ap(x):
        buf, off, _c = PLACE[x[0]]
        if x[3] == 1:
            return T[buf][:, off + x[1]:off + x[2]]
        return T[buf][:, off + x[1]:off + x[2]:x[3]]

    def src(x):
        if x[0] == "@":
            return ap(x[1]).indirect(ap(x[2]))
        return ap(x)

    def rd(x):
        if isinstance(x, tuple):
            return [x[1], x[2]] if x[0] == "@" else [x]
        return []

    def sc(x):
        return ap(x) if isinstance(x, tuple) else x

    def add(q, fn, reads, writes, sem=None, inc=1):
        ops.append({"q": q, "fn": fn, "r": reads, "w": writes, "sem": sem, "inc": inc})

    def at(win, off):
        return ("@", win, off)

    def tt(out, a, b, op):
        add("V", lambda: g.vector.tensor_tensor(ap(out), src(a), ap(b), op), rd(a) + [b], [out])

    def ts(out, a, s1, op0, s2=None, op1=None):
        if op1 is None:
            fn = lambda: g.vector.tensor_scalar(ap(out), src(a), sc(s1), None, op0)
        else:
            fn = lambda: g.vector.tensor_scalar(ap(out), src(a), sc(s1), sc(s2), op0, op1)
        add("V", fn, rd(a) + rd(s1) + rd(s2), [out])

    def cp(out, a):
        add("V", lambda: g.vector.tensor_copy(ap(out), src(a)), rd(a), [out])

    def scatter(win, off, a):
        add("V", lambda: g.vector.tensor_copy(ap(win).indirect(ap(off)), ap(a)), [a, off], [win])

    def scan(out, d0, d1, init, op0, op1):
        add("V", lambda: g.vector.tensor_tensor_scan(ap(out), ap(d0), ap(d1), sc(init), op0, op1), [d0, d1] + rd(init), [out])

    def fill(out, c):
        add("V", lambda: g.vector.memset(ap(out), c), [], [out])

    def quant(qc, qs, x):
        add("V", lambda: g.vector.quantize_mx(ap(qc), ap(qs), ap(x)), [x], [qc, qs])

    def act(out, a, f, bias=None, scale=None, acc=None):
        kw = {}
        if bias is not None:
            kw["bias"] = bias
        if scale is not None:
            kw["scale"] = scale
        if acc is not None:
            kw["accum_out"] = acc
        add("S", lambda: g.scalar.activation(ap(out), src(a), f, **{k: sc(x) for k, x in kw.items()}),
            rd(a) + rd(bias), [out] + rd(acc))

    def iota(out, pat, base, cm):
        if ARENA[PLACE[out[0]][0]][0] == I:
            fn = lambda: g.iota(ap(out), pat, base, cm)
        else:
            fn = lambda: g.iota(ap(out), pat, base, cm, allow_small_or_imprecise_dtypes=True)
        add("G", fn, [], [out])

    def zero(out):
        iota(out, [[0, count(out)]], 0, 0)

    def mm(out, wc, ws, xc, xs, start=True, stop=True):
        add("T", lambda: g.tensor.matmul_mx(ap(out), ap(wc), ap(ws), ap(xc), ap(xs), start, stop), [wc, ws, xc, xs], [out])

    def dma(q, fn, reads, writes, sem):
        e = g.sync if q == "Y" else g.scalar
        add(q, lambda: fn(e), reads, writes, sem, 16)

    def far(out, a, sem, codes):
        if codes:
            fn = lambda: g.remote_dma(ap(out).bitcast(dt.uint8), ap(a).bitcast(dt.uint8), T.sem[sem], T.sem.sent, pid, rid, far_mask)
        else:
            fn = lambda: g.remote_dma(ap(out), ap(a), T.sem[sem], T.sem.sent, pid, rid, far_mask)
        add("G", fn, [a], [out], sem, far_n)

    def wrap(spread, n, tmp):
        scan(v(tmp, 0, n), v("rst", 0, n), spread, 0.0, AL.mult, AL.add)
        return v(tmp, 15, n, 16)

    def part(x, a, b):
        return (x[0], x[1] + a * x[3], min(x[2], x[1] + b * x[3]), x[3])

    def cuts(n):
        h = (n // 32 + 1) // 2 * 32
        return ((0, h), (h, n))

    def masked(out, tmp, a, n):
        for lo, hi in cuts(n):
            tt(v(tmp, lo, hi), part(a, lo, hi), v("mask", lo, hi), AL.mult)
        for lo, hi in cuts(n):
            scan(v(out, lo, hi), v("rst", lo, hi), v(tmp, lo, hi), 0.0, AL.mult, AL.add)
        return v(out, 15, n, 16)

    dma("S", lambda e: e.dma_start(ap(v("pw0", 0, 20)), T.pa[:]), [], [v("pw0", 0, 20)], "lpa")
    dma("Y", lambda e: e.dma_start(ap(v("ut")), T.u[:]), [], [v("ut")], "lu")
    dma("Y", lambda e: e.dma_start(ap(v("x0", 0, 4 * C)), T.x[:]), [], [v("x0", 0, 4 * C)], "lx")
    dma("S", lambda e: e.dma_start(ap(v("nri")), T.nr[:]), [], [v("nri")], "lnr")
    dma("Y", lambda e: e.dma_start(ap(v("wqc")).bitcast(dt.uint8), T.wc[:]), [], [v("wqc")], "lwc")
    dma("Y", lambda e: e.dma_start(ap(v("wqs")), T.ws[:]), [], [v("wqs")], "lws")
    dma("Y", lambda e: e.dma_start(ap(v("vt")), T.v[:]), [], [v("vt")], "lv")

    iota(v("pi"), [[0, 1]], 0, 1)
    iota(v("mod16"), [[0, 32], [1, 16]], 0, 0)
    iota(v("upi"), [[16, 8]], 0, 0)
    iota(v("hit"), [[512, 32], [0, 16]], 0, 0)
    iota(v("plw"), [[16, 32]], 0, 0)
    iota(v("cb"), [[1, 2], [16, 2]], 0, 0)
    iota(v("blk"), [[1, 8], [0, 64]], 0, 0)
    fill(v("ones"), 1.0)
    scan(v("iota"), v("ones"), v("ones"), -257.0, AL.mult, AL.add)
    ts(v("ri"), v("pi"), 15, AL.bitwise_and)
    cp(v("rf"), v("ri"))
    ts(v("gi"), v("pi"), 4, AL.arith_shift_right)
    cp(v("gf"), v("gi"))
    ts(v("mask"), v("mod16"), v("rf"), AL.is_equal)
    ts(v("rst"), v("mod16"), 0.5, AL.is_gt)
    ts(v("offd"), v("mod16"), v("rf"), AL.not_equal, BIG, AL.mult)
    zero(v("r4"))
    ts(v("r4", 0, SL, 4), v("ones", 0, A), HUGE, AL.mult)
    fill(v("hugeb"), HUGE)
    cp(v("upo"), v("upi"))
    for b in range(4):
        add("G", lambda b=b: g.affine_select(ap(v("et%d" % b)), ap(v("ones")), [[-1, 512]], AL.is_equal, 0.0, b, 4),
            [v("ones")], [v("et%d" % b)])
        quant(v("eqc", 128 * b, 128 * b + 128), v("eqs", 128 * b, 128 * b + 128), v("et%d" % b))
    ts(v("bd"), v("blk"), v("gf"), AL.is_equal)
    quant(v("bdqc"), v("bdqs"), v("bd"))
    for t in range(R):
        ts(v("slw", 24 * t, 24 * t + 24), v("plw", 0, 24), v("rf"), AL.add, -256.0, AL.add)
    quant(v("uqc"), v("uqs"), v("ut"))
    add("V", lambda: g.vector.tensor_copy(ap(v("urc")).bitcast(dt.uint32), ap(v("uqc")).bitcast(dt.uint32).indirect(ap(v("upo")))),
        [v("uqc"), v("upo")], [v("urc")])
    add("S", lambda: g.scalar.activation(ap(v("urs")), ap(v("uqs")).indirect(ap(v("upo"))), AF.Copy),
        [v("uqs"), v("upo")], [v("urs")])
    quant(v("vqc"), v("vqs"), v("vt"))

    cp(v("nro"), v("nri"))
    for t in range(R):
        tt(v("key", SL * t, SL * t + SL), at(v("hit"), v("nro", 24 * t, 24 * t + 24)), v("iota", 0, SL), AL.add)
    ts(v("hi1"), v("nri"), 4, AL.arith_shift_right)
    ts(v("hi2"), v("hi1"), -512.0, AL.mult)
    tt(v("nkey"), v("hi2"), v("slw"), AL.subtract)
    ts(v("bkt"), v("cb"), v("rf"), AL.add, -512.0, AL.mult)
    ts(v("bkt"), v("bkt"), 300.0, AL.add)
    for t in range(R):
        ts(v("dum", 2 * t, 2 * t + 2), v("cb", 0, 2), v("rf"), AL.add, 385.0, AL.add)
        for i in range(4):
            col = 4 * (i // 2) + 2 * t + i % 2
            act(v("jc", SL * i, SL * i + SL), v("key", SL * t, SL * t + SL), AF.Sign, bias=v("bkt", i, i + 1),
                acc=v("cnt", col, col + 1))
        a, e = 2 * t, 2 * t + 2
        ts(v("e1", a, e), v("cnt", a, e), 0.5, AL.mult, 191.0, AL.add)
        tt(v("em", a, e), v("cnt", a, e), v("cnt", 4 + a, 4 + e), AL.is_equal)
        tt(v("e2", a, e), v("dum", a, e), v("e1", a, e), AL.subtract)
        tt(v("e3", a, e), v("e2", a, e), v("em", a, e), AL.mult)
        tt(v("e4", a, e), v("e3", a, e), v("e1", a, e), AL.add)
        cp(v("endo", a, e), v("e4", a, e))
    for t in range(R):
        act(v("near%d" % t), at(v("iota"), v("nro", 24 * t, 24 * t + 24)), AF.Identity, bias=256.0)
        for i in range(4):
            act(v("nu%d" % t, i, SL, 4), v("near%d" % t, i, SL, 4), AF.Identity, bias=512.0 * (3 - i))
    zero(v("pw0", 20, 32))
    zero(v("pw1", 24, 32))
    cp(v("po0", 0, 20), v("pw0", 0, 20))

    for t in range(R):
        n = C + A * t
        K = n // 16
        s = str(t)
        m = n + A
        nro = v("nro", 24 * t, 24 * t + 24)
        for c in range(24):
            act(v("js" + s, SL * (c % 6), SL * (c % 6) + SL), v("key", SL * t, SL * t + SL), AF.Sign,
                bias=v("nkey", 24 * t + c, 24 * t + c + 1), acc=v("sg" + s, c, c + 1))
        ts(v("pos" + s), v("sg" + s), 383.0, AL.add, 0.5, AL.mult)
        scatter(v("sw" + s), v("pos" + s), v("iota", 0, SL))
        w = masked("sws" + s, "swm" + s, v("sw" + s), SL)
        ts(v("so" + s), w, 256.0, AL.add)
        ts(v("si" + s), w, 256.0, AL.add)
        ts(v("sh" + s), v("si" + s), 2, AL.arith_shift_right)
        ts(v("do" + s), v("sh" + s), 4.0, AL.mult, 3.0, AL.add)
        act(v("us" + s), at(v("iota"), v("do" + s)), AF.Identity, bias=63.25 + n, scale=0.25)
        zero(v("rr" + s))
        scatter(v("rr" + s, 16, 448), v("endo", 2 * t, 2 * t + 2), v("hugeb"))
        fill(v("fs" + s, SL, 424), BIG)
        zero(v("as" + s, SL, 424))
        zero(v("keep" + s))
        zero(v("hold" + s, n, 512))
        zero(v("rs" + s, 0, 1))
        ts(v("left" + s), v("plw"), -1.0, AL.mult, v("rf"), AL.add)
        tiles = planes_of(n)
        for k, pl in enumerate(tiles):
            lo, hi = width(pl[0], n), max(128, width(pl[3], n))
            zero(v("tl%d%d" % (t, k), 4 * lo, 4 * hi))

        qc, qs = v("q%dc" % t), v("q%ds" % t)
        if t == 0:
            quant(qc, qs, v("x0", 0, 4 * n))
        far(v("l%dc" % t), qc, "ac" + s, True)
        far(v("l%ds" % t), qs, "ac" + s, False)
        mm(bank(4, 0, n), v("urc"), v("urs"), qc, qs)
        mm(bank(7, 0, n), v("urc"), v("urs"), qc, qs)
        cp(v("s" + s), bank(4, 0, n))
        act(v("sp" + s), bank(7, 0, n), AF.Copy)
        for lo, hi in cuts(n):
            tt(v("df" + s, lo, hi), at(v("s" + s), v("po" + s, lo // 16, hi // 16)), v("sp" + s, lo, hi), AL.subtract)
        for lo, hi in cuts(n):
            act(v("ca" + s, lo, hi), v("df" + s, lo, hi), AF.Abs)
            act(v("ce" + s, lo, hi), v("df" + s, lo, hi), AF.Abs)
        tt(v("sm" + s), bank(4, 0, n), v("offd", 0, n), AL.add)
        act(v("sn" + s), at(v("s" + s), nro), AF.Copy)
        act(v("snm" + s), at(v("sm" + s), nro), AF.Copy)
        for b in range(4):
            act(v("xh%d%d" % (t, b), 0, n), v("x" + s, b, 4 * n, 4), AF.Copy, scale=0.5)
            dma("Y", lambda e, b=b, t=t, n=n: e.dma_start(ap(v("xo%d%d" % (b, t), 0, n)), ap(v("xh%d%d" % (t, b), 0, n))),
                [v("xh%d%d" % (t, b), 0, n)], [v("xo%d%d" % (b, t), 0, n)], "xo" + s)
            mm(bank(b, 0, n), v("eqc", 128 * b, 128 * b + 128), v("eqs", 128 * b, 128 * b + 128), v("l%dc" % t), v("l%ds" % t))
            act(v("dp%d%d" % (t, b)), bank(b, 0, n), AF.Copy)

        lst = v("po" + s, 0, K)
        wins = ["wa" + s, "wb" + s, "wc" + s]
        act(v(wins[0]), at(v("iota"), lst), AF.Copy)
        cs = ["ca" + s, "cc" + s, "cd" + s]
        for k, rho in enumerate(RADIX[t]):
            if k + 1 < len(RADIX[t]):
                for j in range(rho - 2):
                    act(v(wins[1]), at(v(wins[0]), lst), AF.Copy)
                    wins = wins[1:] + wins[:1]
                tt(v("gm" + s), at(v(wins[0]), lst), v("mask", 0, n), AL.mult)
                w = wrap(v("gm" + s), n, "gs" + s)
                nxt = v("ql%d%d" % (t, k + 1), 0, K)
                ts(nxt, w, 256.0, AL.add)
                if k + 2 < len(RADIX[t]):
                    act(v(wins[1]), at(v(wins[0]), lst), AF.Copy)
                    wins = wins[1:] + wins[:1]
            if rho == 0:
                for a in range(STEP, n, STEP):
                    tt(v(cs[0], a, a + STEP), at(v(cs[0], 0, a), (lst[0], a // 16, (a + STEP) // 16, 1)), v(cs[0], a, a + STEP), AL.max)
            elif k > 0:
                act(v("ce" + s), v(cs[0]), AF.Copy)
            for j in range(rho - 1):
                tt(v(cs[1]), at(v(cs[0]), lst), v("ce" + s), AL.max)
                cs = cs[1:] + cs[:1]
            if k + 1 < len(RADIX[t]):
                lst = nxt
        c = cs[0]
        act(v("cn" + s), at(v(c), nro), AF.Copy)

        masked("hold" + s, "cm" + s, v(c), n)
        used = 0
        for k in range(len(tiles) - 1, -1, -1):
            tl = "tl%d%d" % (t, k)
            hi = max(128, width(tiles[k][3], n))
            for j in range(3, -1, -1):
                p = tiles[k][j]
                if p == "D":
                    tt(v(tl, j, 4 * n, 4), v(c), v("hold" + s, 0, n), AL.is_lt)
                    dg = wrap(v(tl, j, 4 * n, 4), n, "dgs" + s)
                elif p in BOTH[t]:
                    act(v("jr" + s, used, used + 16 * p), v(c, 0, 16 * p), AF.Sign, bias=v("hold" + s, 16 * p + 15, 16 * p + 16), scale=-1.0)
                    act(v(tl, j, 64 * p, 4), v("jr" + s, used, used + 16 * p), AF.Sign, bias=1.0, acc=v("rs" + s, p, p + 1))
                    used += 16 * p
                elif p is not None:
                    ts(v(tl, j, 64 * p, 4), v(c, 0, 16 * p), v("hold" + s, 16 * p + 15, 16 * p + 16), AL.is_le)
                    act(v("jr" + s, used, used + 16 * p), v(tl, j, 64 * p, 4), AF.Copy, acc=v("rs" + s, p, p + 1))
                    used += 16 * p
            quant(v("tc%d%d" % (t, k)), v("ts%d%d" % (t, k)), v(tl))
            mm(bank(6, 0, hi), v("bdqc"), v("bdqs"), v("tc%d%d" % (t, k)), v("ts%d%d" % (t, k)), k == len(tiles) - 1, k == 0)
        tt(v("r1" + s, 0, K), dg, v("left" + s, 0, K), AL.add)
        tt(v("r2" + s, 0, K), v("r1" + s, 0, K), v("rs" + s, 0, K), AL.add)
        w = masked("cols" + s, "colm" + s, bank(6, 0, n), n)
        tt(v("r3" + s, 0, K), v("r2" + s, 0, K), w, AL.subtract)
        ts(v("rk" + s, 0, K), v("r3" + s, 0, K), n - 16.0, AL.add)
        scatter(v("ew" + s), v("rk" + s, 0, K), v("iota", 0, n))
        tt(v("em" + s), v("ew" + s, 0, A), v("mask", 0, A), AL.mult)
        w = wrap(v("em" + s), A, "ec" + s)
        ts(v("es" + s, 0, 6), w, 256.0, AL.add)
        far(v("el" + s, 0, 6), v("es" + s, 0, 6), "al" + s, False)

        el = v("el" + s, 0, 6)
        for b in range(4):
            o = v("x" + s, 4 * n + b, 4 * m, 4)
            if b % 2 == 0:
                cp(o, at(v("dp%d%d" % (t, b)), el))
            else:
                act(o, at(v("dp%d%d" % (t, b)), el), AF.Copy)
        quant(v("h%dc" % t), v("h%ds" % t), v("x" + s, 4 * (m - 128), 4 * m))
        for b in range(4):
            act(v("xh%d%d" % (t, b), n, m), v("x" + s, 4 * n + b, 4 * m, 4), AF.Copy, scale=0.5)
            act(v("xo%d%d" % (b, t), n, m), v("x" + s, 4 * n + b, 4 * m, 4), AF.Copy, scale=0.5)
        mm(bank(5, 0, 128), v("urc"), v("urs"), v("h%dc" % t), v("h%ds" % t))
        z = bank(5, 128 - A, 128)
        for i in range(4):
            tt(v("d1" + s, i, SL, 4), z, v("sn" + s, i, SL, 4), AL.subtract)
            act(v("gap" + s, i, SL, 4), v("d1" + s, i, SL, 4), AF.Abs)
        for i in range(4):
            tt(v("d2" + s, i, SL, 4), z, v("snm" + s, i, SL, 4), AL.subtract)
        act(v("gaps" + s), at(v("d2" + s), v("so" + s)), AF.Abs)
        for i in range(4):
            tt(v("cost" + s, i, SL, 4), v("gap" + s, i, SL, 4), v("cn" + s, i, SL, 4), AL.max)
        scan(v("f4" + s, 0, SL), v("r4"), v("cost" + s), HUGE, AL.add, AL.min)
        for i in range(1, 4):
            tt(v("keep" + s, i, SL, 4), v("f4" + s, i, SL, 4), v("f4" + s, i - 1, SL, 4), AL.is_equal)
        scan(v("a4" + s), v("keep" + s), v("nu" + s), 0.0, AL.mult, AL.max)
        tt(v("pm" + s), v("a4" + s, 3, SL, 4), v("mask", 0, A), AL.mult)
        w = wrap(v("pm" + s), A, "ps" + s)
        cp(v("pp" + s, 0, 6), w)
        pw = "pw%d" % (t + 1)
        ts(v(pw, K, K + 6), v("pp" + s, 0, 6), 511, AL.bitwise_and)
        for lo, hi in cuts(SL):
            tt(v("price" + s, lo, hi), at(v("f4" + s, 0, SL), v("do" + s, lo // 16, hi // 16)), v("gaps" + s, lo, hi), AL.max)
        for lo, hi in cuts(SL):
            scan(v("fs" + s, lo, hi), v("rr" + s, 15 + lo, 15 + hi), v("price" + s, lo, hi), v("fs" + s, lo - 1, lo) if lo else HUGE,
                 AL.add, AL.min)
            tt(v("nf" + s, lo, hi), v("price" + s, lo, hi), v("fs" + s, lo, hi), AL.not_equal)
            scan(v("as" + s, lo, hi), v("nf" + s, lo, hi), v("us" + s, lo, hi), v("as" + s, lo - 1, lo) if lo else 0.0, AL.mult, AL.max)
        end = v("endo", 2 * t, 2 * t + 2)
        tt(v("mv" + s), at(v("fs" + s), end), v("hold" + s, 15, 512, 16), AL.is_lt)
        tt(v("dl" + s), at(v("as" + s), end), v("pw" + s), AL.subtract)
        tt(v("dm" + s, 0, K), v("dl" + s, 0, K), v("mv" + s, 0, K), AL.mult)
        tt(v(pw, 0, K), v("dm" + s, 0, K), v("pw" + s, 0, K), AL.add)
        po = "po%d" % (t + 1)
        cp(v(po, 0, K + 6), v(pw, 0, K + 6))

        nx = "x%d" % (t + 1)
        for h, (a, e) in enumerate(CHUNKS[t]):
            for b in range(4):
                tt(v("yt" + s, 4 * a + b, 4 * e, 4), at(v("xh%d%d" % (t, b)), v(po, a // 16, e // 16)), v("xo%d%d" % (b, t), a, e), AL.add)
            quant(v("yq%dc" % t, a, e), v("yq%ds" % t, a, e), v("yt" + s, 4 * a, 4 * e))
            for b in range(4):
                k = 4 * h + b
                mm(bank(k, 0, e - a), v("wqc", 128 * b, 128 * b + 128), v("wqs", 128 * b, 128 * b + 128),
                   v("yq%dc" % t, a, e), v("yq%ds" % t, a, e))
                act(v("rl%d%d" % (b, t), a, e), bank(k, 0, e - a), AF.Relu, scale=0.03125)
                tt(v(nx, 4 * a + b, 4 * e, 4), v("rl%d%d" % (b, t), a, e), v("x" + s, 4 * a + b, 4 * e, 4), AL.add)
            quant(v("q%dc" % (t + 1), a, e), v("q%ds" % (t + 1), a, e), v(nx, 4 * a, 4 * e))

    act(v("opr"), at(v("iota"), v("po2")), AF.Identity, bias=256.0)
    ob, oo, _c = PLACE["opr"]
    for k in range(8):
        dma("Y", lambda e, k=k: e.dma_start(T.op[k:k + 1, :], T[ob][16 * k:16 * k + 1, oo:oo + 512]), [v("opr")], [], "out")
    for h, (a, e) in enumerate(CHUNKS[R - 1]):
        dma("Y", lambda q, a=a, e=e: q.dma_start(T.oc[:, 4 * a:4 * e], ap(v("q2c", a, e)).bitcast(dt.uint8)), [v("q2c", a, e)], [], "out")
        for k in range(4):
            dma("Y" if h == 0 or k < 2 else "S",
                lambda q, a=a, e=e, k=k: q.dma_start(T.osc[4 * k:4 * k + 4, a:e], T.q2s[32 * k:32 * k + 4, a:e]),
                [v("q2s", a, e)], [], "out")
        mm(bank(4 * h, 0, e - a), v("vqc"), v("vqs"), v("q2c", a, e), v("q2s", a, e))
        act(v("ysb", a, e), bank(4 * h, 0, e - a), AF.Copy)
        dma("S", lambda q, a=a, e=e: q.dma_start(T.y[:, a:e], ap(v("ysb", a, e))), [v("ysb", a, e)], [], "out")
    return ops


def depend(ops):
    wr, rdrs = {}, {}
    for i, o in enumerate(ops):
        deps = set()
        touched = []
        for kind in ("r", "w"):
            for x in o[kind]:
                buf, off, _c = PLACE[x[0]]
                if buf == "acc":
                    cells = [("acc", x[1] // 512)]
                else:
                    cells = [(buf, off + j) for j in range(x[1], x[2], x[3])]
                touched.append((kind, buf, cells))
        for kind, buf, cells in touched:
            for cell in cells:
                if cell in wr:
                    deps.add(wr[cell])
                if kind == "w":
                    deps.update(rdrs.get(cell, ()))
                elif buf == "acc":
                    deps.update(j for j in rdrs.get(cell, ()) if ops[j]["q"] != o["q"])
        for kind, buf, cells in touched:
            for cell in cells:
                if kind == "w":
                    wr[cell] = i
                    rdrs[cell] = []
        for kind, buf, cells in touched:
            if kind == "r":
                for cell in cells:
                    if wr.get(cell) != i:
                        rdrs.setdefault(cell, []).append(i)
        deps.discard(i)
        o["deps"] = sorted(deps)


ORDER = [
    0,1,9,25,394,2,3,123,6,7,14,4,5,11,18,10,15,16,19,26,17,38,37,399,128,13,85,39,166,43,8,46,40,47,134,41,44,167,138,12,137,33,48,140,42,21,171,139,62,49,141,89,27,35,86,142,20,88,51,50,168,29,143,144,36,146,169,145,170,91,172,83,174,31,173,90,175,87,23,22,179,176,93,180,121,178,28,177,181,92,129,24,182,147,32,30,187,34,132,183,188,133,94,184,398,95,126,189,96,124,185,392,98,190,99,186,191,97,192,130,193,102,194,400,195,201,105,196,101,197,203,198,402,245,108,249,251,199,235,239,107,202,135,247,231,250,204,252,406,103,237,241,205,104,127,136,211,240,236,215,84,100,209,131,219,248,207,212,125,217,106,213,210,221,396,214,227,208,229,223,218,225,224,403,243,238,233,228,45,230,234,401,232,244,226,253,206,216,254,405,255,220,257,258,242,404,160,259,222,260,156,246,397,149,256,152,395,261,262,164,109,263,52,73,110,264,165,265,266,157,111,267,148,161,53,55,56,112,54,113,153,114,57,115,58,158,117,59,116,118,60,119,61,159,271,270,269,268,200,272,122,281,74,282,284,278,286,76,288,290,283,291,292,287,295,289,285,297,162,298,296,274,293,163,77,299,294,300,301,150,308,120,309,151,310,302,154,311,75,155,78,313,303,314,357,312,362,304,315,316,280,305,317,275,306,276,318,273,307,319,279,320,277,339,438,340,81,342,80,79,439,321,341,360,322,343,443,440,344,350,82,345,347,323,351,353,324,358,441,325,348,352,359,332,329,442,349,354,326,335,330,346,333,327,331,446,334,328,336,355,361,337,364,356,365,338,447,408,410,363,450,409,407,448,449,411,412,454,413,414,415,455,416,418,417,456,458,444,367,457,445,366,419,451,436,462,452,424,463,428,453,432,464,459,369,460,370,371,461,368,465,467,466,374,468,376,372,469,373,470,375,471,378,472,377,380,473,63,474,379,64,381,476,65,477,429,478,479,524,486,500,510,496,490,480,497,501,494,511,504,482,495,514,487,484,483,492,506,515,488,491,502,493,489,512,498,525,485,526,516,499,508,505,520,527,509,530,503,518,522,513,519,532,536,534,528,521,540,538,537,529,517,542,67,544,533,539,481,535,69,545,531,546,543,523,548,541,549,507,550,551,426,547,552,66,553,427,554,421,425,420,68,555,70,437,556,71,557,382,558,430,475,431,434,72,384,433,435,383,422,386,385,393,388,423,387,389,390,561,562,559,560,571,563,570,566,572,568,565,575,564,579,577,576,573,582,578,581,574,583,587,580,588,569,567,586,589,584,590,585,593,591,391,599,600,601,592,602,604,603,605,594,606,595,608,607,596,609,597,610,598,611,613,648,612,614,655,656,654,652,649,615,650,651,653,631,616,630,617,626,632,618,623,627,633,620,624,619,621,634,628,638,635,625,639,641,636,622,644,642,640,645,637,643,646,629,647,657,662,658,659,666,669,670,660,668,665,663,667,661,671,664,672]

PLAN = {}


def rank_program(g, core, T, topo):
    rank = T.rank_of(core)
    if rank is None:
        return
    ops = build(g, T, topo, (core, T.cores[(rank + 1) % len(T.cores)]))
    if not PLAN:
        depend(ops)
        PLAN["deps"] = [o["deps"] for o in ops]
    queue = {"V": g.vector, "S": g.scalar, "T": g.tensor, "G": g, "Y": g.sync}
    total = {}
    for o in ops:
        if o["sem"] is not None:
            total[o["sem"]] = total.get(o["sem"], 0) + o["inc"]
    done = {}
    for i, o in enumerate(ops):
        if o["sem"] is not None:
            done[i] = (o["sem"], total[o["sem"]])
    seen = {q: {} for q in queue}
    sent = 0
    for i in ORDER:
        o = ops[i]
        q = o["q"]
        need = {}
        for d in PLAN["deps"][i]:
            sem, val = done[d]
            need[sem] = max(need.get(sem, 0), val)
        for sem in need:
            if seen[q].get(sem, 0) < need[sem]:
                queue[q].wait_ge(T.sem[sem], need[sem])
                seen[q][sem] = need[sem]
        ins = o["fn"]()
        if o["sem"] is None:
            sem = "c" + q
            total[sem] = total.get(sem, 0) + 1
            ins.then_inc(T.sem[sem], 1)
            done[i] = (sem, total[sem])
        elif o["sem"] in FAR:
            sent += o["inc"]
        else:
            ins.then_inc(T.sem[o["sem"]], 16)
    total["sent"] = sent
    for sem in total:
        if seen["G"].get(sem, 0) < total[sem]:
            g.wait_ge(T.sem[sem], total[sem])
